import numpy as np
import ml_dtypes


def mxq(x, axis, fmt="e4m3"):
    dtype, down = {"e4m3": (ml_dtypes.float8_e4m3fn, 7), "e5m2": (ml_dtypes.float8_e5m2, 14)}[fmt]
    v = np.moveaxis(np.asarray(x, np.float32).astype(ml_dtypes.bfloat16).astype(np.float64), axis, -1)
    blocks = v.reshape(v.shape[:-1] + (-1, 32))
    amax = np.abs(blocks).max(-1, keepdims=True)
    byte = np.maximum(np.where(amax > 0, np.frexp(amax)[1] - 1 + 127, 0) - down, 1)
    scale = np.exp2(byte - 127.0)
    codes = (blocks / scale).astype(np.float32).astype(dtype).astype(np.float64)
    return np.moveaxis((codes * scale).reshape(v.shape), -1, axis)


WIDE = False


def mx_kscale(k):
    if not WIDE:
        return np.ones(k)
    levels = np.array([10, -10, 5, -5, 0])
    if k % 512:
        return np.exp2(np.random.permutation(np.resize(levels, k // 32))).repeat(32)
    a = np.empty((k // 512, 16))
    for p in range(k // 512):
        a[p, :8] = np.random.permutation(np.resize(levels, 8))
        for g in range(8):
            far = levels[np.abs(levels - a[p, g]) >= 10]
            a[p, g + 8] = far[np.random.randint(len(far))]
    return np.exp2(a.ravel()).repeat(32)


def f64(x):
    return np.asarray(x).astype(np.float64)


def striped(idx):
    return np.tile(idx.reshape(-1, 16).T, (8, 1)).astype(np.uint16)


def unstriped(offs):
    return offs[:16].T.reshape(-1).astype(np.int64)


def pack_weight(w):
    k, n = w.shape
    w = f64(np.asarray(w, np.float32).astype(ml_dtypes.bfloat16)).reshape(k // 32, 32, n)
    amax = np.abs(w).max(1)
    byte = np.clip(np.where(amax > 0, np.frexp(amax)[1] - 1 + 127 - 7, 1), 1, 254)
    scaled = (w * np.exp2(127.0 - byte)[:, None, :]).reshape(k, n).astype(np.float32)
    words = np.ascontiguousarray(scaled.reshape(k // 512, 128, 4, n).transpose(0, 1, 3, 2)).astype(ml_dtypes.float8_e4m3fn).view(np.uint8)
    return words, np.ascontiguousarray(byte.astype(np.uint8).reshape(k // 512, 16, n))


def unpack_weight(words, scales):
    g, p, n, _ = words.shape
    vals = np.ascontiguousarray(words).view(ml_dtypes.float8_e4m3fn).astype(np.float64) * np.repeat(np.exp2(scales.astype(np.float64) - 127.0), 8, axis=1)[..., None]
    return vals.transpose(0, 1, 3, 2).reshape(g * 512, n)


E2M1 = np.array([0.0, 0.5, 1.0, 1.5, 2.0, 3.0, 4.0, 6.0, -0.0, -0.5, -1.0, -1.5, -2.0, -3.0, -4.0, -6.0])


def pack_fp4(w):
    k, n = w.shape
    w = f64(np.asarray(w, np.float32).astype(ml_dtypes.bfloat16)).reshape(k // 32, 32, n)
    amax = np.abs(w).max(1)
    mant, ex = np.frexp(amax / 6.0)
    byte = np.clip(np.where(amax > 0, np.where(mant > 0.5, ex, ex - 1) + 127, 1), 1, 254)
    scaled = (w * np.exp2(127.0 - byte)[:, None, :]).reshape(k, n).astype(np.float32)
    c = np.ascontiguousarray(scaled.reshape(k // 512, 128, 4, n).transpose(0, 1, 3, 2)).astype(ml_dtypes.float4_e2m1fn).view(np.uint8) & 0xF
    words = (c[..., 0::2] | (c[..., 1::2] << 4)).reshape(k // 512, 128, 2 * n)
    return np.ascontiguousarray(words), np.ascontiguousarray(byte.astype(np.uint8).reshape(k // 512, 16, n))


def unpack_fp4(words, scales):
    g, _, n = scales.shape
    words = np.ascontiguousarray(words).reshape(g, 128, n, 2)
    nib = np.empty((g, 128, n, 4), np.uint8)
    nib[..., 0::2] = words & 0xF
    nib[..., 1::2] = words >> 4
    vals = E2M1[nib] * np.repeat(np.exp2(scales.astype(np.float64) - 127.0), 8, axis=1)[..., None]
    return vals.transpose(0, 1, 3, 2).reshape(g * 512, n)


def relu(v):
    return np.maximum(v, 0.0)


def gelu(v):
    return 0.5 * v * (1.0 + np.tanh(np.sqrt(2.0 / np.pi) * (v + 0.044715 * v**3)))


K, T, S, D, V, H, N, U = 512, 2048, 1024, 3, 512, 512, 128, 256
P = 2 ** 7


def setup_inputs():
    n = np.random.standard_normal
    s = mx_kscale(K)[:, None]
    u = mx_kscale(H)
    packed_xT = pack_weight(n((K, T)) * s)
    packed_w2 = pack_fp4(n((H, N)) / np.sqrt(H) / u[:, None])
    return {
        "x_words": packed_xT[0],
        "x_scales": packed_xT[1],
        "w1": (n((K, H)) / np.sqrt(K) / s * u).astype(np.float32),
        "w2_words": packed_w2[0],
        "w2_scales": packed_w2[1],
        "gate": (np.tile(np.random.uniform(0.2, 1.0, (D, 1, V)) / np.sqrt(D), (1, P, 1))).astype(np.float32),
        "gate2": (np.tile(np.random.uniform(0.2, 1.0, (D, 1, U)) / np.sqrt(D), (1, P, 1))).astype(np.float32),
        "offs": striped(np.random.permutation(T)[:S]),
        "pos1": striped(np.random.permutation(S)[:V]),
        "pos2": striped(np.random.permutation(S)[:V]),
        "pos3": striped(np.random.permutation(S)[:V]),
        "nxt1": striped(np.random.permutation(V)[:U]),
        "nxt2": striped(np.random.permutation(V)[:U]),
        "nxt3": striped(np.random.permutation(V)[:U]),
    }


def reference(x_words, x_scales, w1, w2_words, w2_scales, gate, gate2, offs, pos1, pos2, pos3, nxt1, nxt2, nxt3):
    xq = unpack_weight(x_words, x_scales)[:, unstriped(offs)]
    h = gelu(mxq(f64(w1), 0, "e4m3").T @ xq)
    z = h[:, unstriped(pos1)] * f64(gate)[0, :1] + h[:, unstriped(pos2)] * f64(gate)[1, :1] + h[:, unstriped(pos3)] * f64(gate)[2, :1]
    g = relu(unpack_fp4(w2_words, w2_scales).T @ mxq(z, 0, "e4m3"))
    return g[:, unstriped(nxt1)] * f64(gate2)[0, :1] + g[:, unstriped(nxt2)] * f64(gate2)[1, :1] + g[:, unstriped(nxt3)] * f64(gate2)[2, :1]

@@ -1,0 +1,211 @@
+from contextlib import ExitStack
+
+import concourse.mybir as mybir
+from concourse.masks import make_identity
+
+K, T, S, D, V, H, N, U = 512, 2048, 1024, 3, 512, 512, 128, 256
+FLOPS = 2 * K * H * S + 2 * H * N * V
+
+F32 = mybir.dt.float32
+BF16 = mybir.dt.bfloat16
+I32 = mybir.dt.int32
+U32 = mybir.dt.uint32
+U16 = mybir.dt.uint16
+U8 = mybir.dt.uint8
+FP8X4 = mybir.dt.float8_e4m3fn_x4
+FP4X4 = mybir.dt.float4_e2m1fn_x4
+MULT = mybir.AluOpType.mult
+ADD = mybir.AluOpType.add
+GELU = mybir.ActivationFunctionType.Gelu_apprx_tanh
+RELU = mybir.ActivationFunctionType.Relu
+
+P = 128
+PACK = 4
+LIST_ROWS = 16
+BLOCKS = H // P
+PICK_PIECES = ((0, 512), (512, 768), (768, 1024))
+Z_CHUNKS = ((0, 256), (256, 384), (384, 512))
+
+
+def entries(list_tile, lo, hi):
+    return list_tile[:, lo // LIST_ROWS : hi // LIST_ROWS]
+
+
+def load_scale_rows(queue, plane, rows):
+    for q in range(4):
+        queue.dma_start(out=plane[32 * q : 32 * q + 4, :].bitcast(I32), in_=rows[4 * q : 4 * q + 4, :].bitcast(I32))
+
+
+def tile_picked_hop2_gelu_p_kernel(
+    tc, x_words, x_scales, w1, w2_words, w2_scales, gate, gate2, offs, pos1, pos2, pos3, nxt1, nxt2, nxt3, out
+):
+    nc = tc.nc
+    with ExitStack() as ctx:
+        keep = ctx.enter_context(tc.tile_pool(name="keep", bufs=1))
+        psum = ctx.enter_context(tc.psum_pool(name="psum", bufs=1))
+
+        def sbuf(name, shape, dtype):
+            return keep.tile(shape, dtype, name=name, align_bytes=64)
+
+        offs_sb = sbuf("offs_sb", [P, S // LIST_ROWS], U16)
+        pos_sb = [sbuf("pos_sb%d" % d, [P, V // LIST_ROWS], U16) for d in range(D)]
+        nxt_sb = [sbuf("nxt_sb%d" % d, [P, U // LIST_ROWS], U16) for d in range(D)]
+        x_table = sbuf("x_table", [P, T], I32)
+        x_scale_table = sbuf("x_scale_table", [P, T], U8)
+        w1_first = sbuf("w1_first", [P, PACK, P], F32)
+        w1_rest = sbuf("w1_rest", [P, PACK, H - P], F32)
+        gate_first = sbuf("gate_first", [P, V], F32)
+        gate_rest = sbuf("gate_rest", [P, D - 1, V], F32)
+        gate2_sb = sbuf("gate2_sb", [P, D, U], F32)
+        w2_codes = sbuf("w2_codes", [P, 2 * N], U8)
+        w2_plane = sbuf("w2_plane", [P, N], U8)
+        identity = sbuf("identity", [P, P], F32)
+        warm_in = sbuf("warm_in", [P, 8], F32)
+        warm_out = sbuf("warm_out", [P, 8], F32)
+
+        nc.gpsimd.memset(x_scale_table[:].bitcast(I32), 0)
+        nc.vector.memset(warm_in[:], 0.0)
+        w1_rows = w1.rearrange("(p j) c -> p j c", j=PACK)
+        nc.sync.dma_start(offs_sb[:], offs)
+        nc.sync.dma_start(out=w1_first[:], in_=w1_rows[:, :, 0:P])
+        nc.sync.dma_start(out=x_table[:], in_=x_words[0].rearrange("p n t -> p (n t)").bitcast(I32))
+        load_scale_rows(nc.scalar, x_scale_table, x_scales[0])
+        nc.scalar.activation(warm_out[:], warm_in[:], GELU)
+        nc.sync.dma_start(out=w1_rest[:], in_=w1_rows[:, :, P:H])
+        nc.sync.dma_start(out=gate_first[:], in_=gate[0])
+        nc.sync.dma_start(pos_sb[0][:], pos1)
+        nc.sync.dma_start(out=gate_rest[:], in_=gate[1:D].rearrange("d p v -> p d v"))
+        nc.sync.dma_start(pos_sb[1][:], pos2)
+        nc.sync.dma_start(pos_sb[2][:], pos3)
+        make_identity(nc, identity[:])
+        nc.gpsimd.memset(w2_plane[:], 0)
+        nc.sync.dma_start(out=w2_codes[:].bitcast(I32), in_=w2_words[0].bitcast(I32))
+        load_scale_rows(nc.sync, w2_plane, w2_scales[0])
+        nc.sync.dma_start(out=gate2_sb[:], in_=gate2.rearrange("d p u -> p d u"))
+        for tile, source in zip(nxt_sb, (nxt1, nxt2, nxt3)):
+            nc.sync.dma_start(tile[:], source)
+        gate_rows = [gate_first[:]] + [gate_rest[:, d, :] for d in range(D - 1)]
+
+        w1_bf16 = [sbuf("w1_bf16_%d" % b, [P, P, PACK], BF16) for b in range(BLOCKS)]
+        w1_codes = [sbuf("w1_codes%d" % b, [P, P], U32) for b in range(BLOCKS)]
+        w1_plane = [sbuf("w1_plane%d" % b, [P, P], U8) for b in range(BLOCKS)]
+
+        def round_w1(b, copy):
+            raw = w1_first[:] if b == 0 else w1_rest[:, :, (b - 1) * P : b * P]
+            copy(
+                out=w1_bf16[b][:].rearrange("p (c i) j -> p c j i", i=4),
+                in_=raw.rearrange("p j (c i) -> p c j i", i=4),
+            )
+
+        def quantize_w1(b):
+            nc.vector.quantize_mx(
+                out=w1_codes[b][:].bitcast(FP8X4),
+                scales=w1_plane[b][:],
+                in_=w1_bf16[b][:].rearrange("p c j -> p (c j)"),
+            )
+
+        picked_plane = sbuf("picked_plane", [P, S], U8)
+        picked_codes = sbuf("picked_codes", [P, S], U32)
+        h = [sbuf("h%d" % b, [P, S], F32) for b in range(BLOCKS)]
+
+        def first_layer(b, lo, hi):
+            acc = psum.tile([P, hi - lo], F32, name="product", tag="product", bufs=3)
+            nc.tensor.matmul_mx(
+                out=acc[:],
+                lhsT=w1_codes[b][:].bitcast(FP8X4),
+                lhsT_scale=w1_plane[b][:],
+                rhs=picked_codes[:, lo:hi].bitcast(FP8X4),
+                rhs_scale=picked_plane[:, lo:hi],
+                start=True,
+                stop=True,
+            )
+            nc.scalar.activation(h[b][:, lo:hi], acc[:], GELU)
+
+        nc.vector.tensor_copy(picked_plane[:], x_scale_table[:].indirect(offs_sb[:]))
+        round_w1(0, nc.scalar.copy)
+        quantize_w1(0)
+        for lo, hi in PICK_PIECES:
+            nc.vector.tensor_copy(picked_codes[:, lo:hi], x_table[:].bitcast(U32).indirect(entries(offs_sb, lo, hi)))
+            first_layer(0, lo, hi)
+        round_w1(1, nc.vector.tensor_copy)
+        quantize_w1(1)
+        for b in range(2, BLOCKS):
+            round_w1(b, nc.scalar.copy)
+
+        z_rows = [sbuf("z_rows%d" % c, [P, (hi - lo) // P, 2, P, 2], BF16) for c, (lo, hi) in enumerate(Z_CHUNKS)]
+
+        def gather_terms(b, lo, hi):
+            terms = []
+            for d in range(D):
+                term = sbuf("term_%d_%d_%d" % (b, lo, d), [P, hi - lo], F32)
+                nc.vector.tensor_tensor(term[:], h[b][:].indirect(entries(pos_sb[d], lo, hi)), gate_rows[d][:, lo:hi], MULT)
+                terms.append(term)
+            return terms
+
+        def sum_and_turn(b, terms, lo, hi):
+            total = psum.tile([P, (hi - lo) // P, P], F32, name="total", tag="total", bufs=3)
+            for n in range((hi - lo) // P):
+                for d in range(D):
+                    nc.tensor.matmul(
+                        total[:, n, :], terms[d][:, n * P : (n + 1) * P], identity[:],
+                        start=(d == 0), stop=(d == D - 1), is_transpose=True,
+                    )
+            for c, (c_lo, c_hi) in enumerate(Z_CHUNKS):
+                if lo <= c_lo and c_hi <= hi:
+                    part = total[:, (c_lo - lo) // P : (c_hi - lo) // P, :]
+                    nc.scalar.copy(
+                        out=z_rows[c][:, :, :, 32 * b : 32 * (b + 1), :],
+                        in_=part.rearrange("v n (m u e) -> v n u m e", u=2, e=2),
+                    )
+
+        g = sbuf("g", [P, V], F32)
+
+        def second_layer(c):
+            lo, hi = Z_CHUNKS[c]
+            tiles = (hi - lo) // P
+            pairs = z_rows[c][:].rearrange("v n u q e -> v (n u q e)").bitcast(F32)
+            turned = psum.tile([P, tiles, 2, P], F32, name="turned", tag="turned", bufs=2)
+            for n in range(tiles):
+                for u in range(2):
+                    nc.tensor.transpose(turned[:, n, u, :], pairs[:, (2 * n + u) * P : (2 * n + u + 1) * P], identity[:])
+            z_bf16 = sbuf("z_bf16_%d" % c, [P, PACK * (hi - lo)], BF16)
+            nc.scalar.copy(
+                out=z_bf16[:].bitcast(F32).rearrange("q (n v u) -> q n v u", n=tiles, u=2),
+                in_=turned[:].rearrange("q n u v -> q n v u"),
+            )
+            z_codes = sbuf("z_codes%d" % c, [P, hi - lo], U32)
+            z_plane = sbuf("z_plane%d" % c, [P, hi - lo], U8)
+            nc.vector.quantize_mx(out=z_codes[:].bitcast(FP8X4), scales=z_plane[:], in_=z_bf16[:])
+            acc = psum.tile([P, hi - lo], F32, name="product", tag="product", bufs=3)
+            nc.tensor.matmul_mx(
+                out=acc[:],
+                lhsT=w2_codes[:].bitcast(FP4X4),
+                lhsT_scale=w2_plane[:],
+                rhs=z_codes[:].bitcast(FP8X4),
+                rhs_scale=z_plane[:],
+                start=True,
+                stop=True,
+            )
+            nc.scalar.activation(g[:, lo:hi], acc[:], RELU)
+
+        for b in range(BLOCKS - 1):
+            for lo in range(0, S, 512):
+                first_layer(b + 1, lo, lo + 512)
+            if b + 2 < BLOCKS:
+                quantize_w1(b + 2)
+            sum_and_turn(b, gather_terms(b, 0, V), 0, V)
+        for c, (lo, hi) in enumerate(Z_CHUNKS):
+            sum_and_turn(BLOCKS - 1, gather_terms(BLOCKS - 1, lo, hi), lo, hi)
+            second_layer(c)
+
+        roots = [sbuf("root_term%d" % d, [P, U], F32) for d in range(D)]
+        for d in range(D):
+            nc.vector.tensor_tensor(roots[d][:], g[:].indirect(nxt_sb[d][:]), gate2_sb[:, d, :], MULT)
+        halves = [slice(0, U // 2), slice(U // 2, U)]
+        partial = sbuf("partial", [P, U], F32)
+        result = [sbuf("result%d" % n, [P, U // 2], F32) for n in range(2)]
+        for cols in halves:
+            nc.vector.tensor_tensor(partial[:, cols], roots[0][:, cols], roots[1][:, cols], ADD)
+        for n, cols in enumerate(halves):
+            nc.vector.tensor_tensor(result[n][:], partial[:, cols], roots[2][:, cols], ADD)
+            (nc.scalar, nc.sync)[n].dma_start(out=out[:, cols], in_=result[n][:])

@@ -31,9 +31,9 @@ def entries(list_tile, lo, hi):
     return list_tile[:, lo // LIST_ROWS : hi // LIST_ROWS]
 
 
-def load_scale_rows(queue, plane, rows):
+def load_scale_rows(queues, plane, rows):
     for q in range(4):
-        queue.dma_start(out=plane[32 * q : 32 * q + 4, :].bitcast(I32), in_=rows[4 * q : 4 * q + 4, :].bitcast(I32))
+        queues[q % len(queues)].dma_start(out=plane[32 * q : 32 * q + 4, :].bitcast(I32), in_=rows[4 * q : 4 * q + 4, :].bitcast(I32))
 
 
 def tile_picked_hop2_gelu_p_kernel(
@@ -44,14 +44,14 @@ def tile_picked_hop2_gelu_p_kernel(
         keep = ctx.enter_context(tc.tile_pool(name="keep", bufs=1))
         psum = ctx.enter_context(tc.psum_pool(name="psum", bufs=1))
 
-        def sbuf(name, shape, dtype):
-            return keep.tile(shape, dtype, name=name, align_bytes=64)
+        def sbuf(name, shape, dtype, tag=None):
+            return keep.tile(shape, dtype, name=name, tag=tag or name, align_bytes=64)
 
         offs_sb = sbuf("offs_sb", [P, S // LIST_ROWS], U16)
         pos_sb = [sbuf("pos_sb%d" % d, [P, V // LIST_ROWS], U16) for d in range(D)]
         nxt_sb = [sbuf("nxt_sb%d" % d, [P, U // LIST_ROWS], U16) for d in range(D)]
-        x_table = sbuf("x_table", [P, T], I32)
-        x_scale_table = sbuf("x_scale_table", [P, T], U8)
+        x_table = sbuf("x_table", [P, T], I32, "after_words")
+        x_scale_table = sbuf("x_scale_table", [P, T], U8, "after_scales")
         w1_first = sbuf("w1_first", [P, PACK, P], F32)
         w1_rest = sbuf("w1_rest", [P, PACK, H - P], F32)
         gate_first = sbuf("gate_first", [P, V], F32)
@@ -63,13 +63,13 @@ def tile_picked_hop2_gelu_p_kernel(
         warm_in = sbuf("warm_in", [P, 8], F32)
         warm_out = sbuf("warm_out", [P, 8], F32)
 
-        nc.gpsimd.memset(x_scale_table[:].bitcast(I32), 0)
+        nc.vector.memset(x_scale_table[:].bitcast(I32), 0)
         nc.vector.memset(warm_in[:], 0.0)
         w1_rows = w1.rearrange("(p j) c -> p j c", j=PACK)
         nc.sync.dma_start(offs_sb[:], offs)
         nc.sync.dma_start(out=w1_first[:], in_=w1_rows[:, :, 0:P])
+        load_scale_rows((nc.sync, nc.scalar), x_scale_table, x_scales[0])
         nc.sync.dma_start(out=x_table[:], in_=x_words[0].rearrange("p n t -> p (n t)").bitcast(I32))
-        load_scale_rows(nc.scalar, x_scale_table, x_scales[0])
         nc.scalar.activation(warm_out[:], warm_in[:], GELU)
         nc.sync.dma_start(out=w1_rest[:], in_=w1_rows[:, :, P:H])
         nc.sync.dma_start(out=gate_first[:], in_=gate[0])
@@ -80,17 +80,18 @@ def tile_picked_hop2_gelu_p_kernel(
         make_identity(nc, identity[:])
         nc.gpsimd.memset(w2_plane[:], 0)
         nc.sync.dma_start(out=w2_codes[:].bitcast(I32), in_=w2_words[0].bitcast(I32))
-        load_scale_rows(nc.sync, w2_plane, w2_scales[0])
+        load_scale_rows((nc.sync,), w2_plane, w2_scales[0])
         nc.sync.dma_start(out=gate2_sb[:], in_=gate2.rearrange("d p u -> p d u"))
         for tile, source in zip(nxt_sb, (nxt1, nxt2, nxt3)):
             nc.sync.dma_start(tile[:], source)
         gate_rows = [gate_first[:]] + [gate_rest[:, d, :] for d in range(D - 1)]
 
-        w1_bf16 = [sbuf("w1_bf16_%d" % b, [P, P, PACK], BF16) for b in range(BLOCKS)]
-        w1_codes = [sbuf("w1_codes%d" % b, [P, P], U32) for b in range(BLOCKS)]
+        w1_bf16 = {}
+        w1_codes = {}
         w1_plane = [sbuf("w1_plane%d" % b, [P, P], U8) for b in range(BLOCKS)]
 
         def round_w1(b, copy):
+            w1_bf16[b] = sbuf("w1_bf16_%d" % b, [P, P, PACK], BF16, "after_words" if b > 0 else None)
             raw = w1_first[:] if b == 0 else w1_rest[:, :, (b - 1) * P : b * P]
             copy(
                 out=w1_bf16[b][:].rearrange("p (c i) j -> p c j i", i=4),
@@ -98,6 +99,7 @@ def tile_picked_hop2_gelu_p_kernel(
             )
 
         def quantize_w1(b):
+            w1_codes[b] = sbuf("w1_codes%d" % b, [P, P], U32, "after_scales" if b == 0 else None)
             nc.vector.quantize_mx(
                 out=w1_codes[b][:].bitcast(FP8X4),
                 scales=w1_plane[b][:],
@@ -129,8 +131,6 @@ def tile_picked_hop2_gelu_p_kernel(
             first_layer(0, lo, hi)
         round_w1(1, nc.vector.tensor_copy)
         quantize_w1(1)
-        for b in range(2, BLOCKS):
-            round_w1(b, nc.scalar.copy)
 
         z_rows = [sbuf("z_rows%d" % c, [P, (hi - lo) // P, 2, P, 2], BF16) for c, (lo, hi) in enumerate(Z_CHUNKS)]
 
@@ -192,6 +192,7 @@ def tile_picked_hop2_gelu_p_kernel(
             for lo in range(0, S, 512):
                 first_layer(b + 1, lo, lo + 512)
             if b + 2 < BLOCKS:
+                round_w1(b + 2, nc.scalar.copy)
                 quantize_w1(b + 2)
             sum_and_turn(b, gather_terms(b, 0, V), 0, V)
         for c, (lo, hi) in enumerate(Z_CHUNKS):

@@ -111,7 +111,7 @@ def tile_picked_hop2_gelu_p_kernel(
         h = [sbuf("h%d" % b, [P, S], F32) for b in range(BLOCKS)]
 
         def first_layer(b, lo, hi):
-            acc = psum.tile([P, hi - lo], F32, name="product", tag="product", bufs=3)
+            acc = psum.tile([P, hi - lo], F32, name="product", tag="product", bufs=4)
             nc.tensor.matmul_mx(
                 out=acc[:],
                 lhsT=w1_codes[b][:].bitcast(FP8X4),
@@ -132,72 +132,80 @@ def tile_picked_hop2_gelu_p_kernel(
         round_w1(1, nc.vector.tensor_copy)
         quantize_w1(1)
 
-        z_rows = [sbuf("z_rows%d" % c, [P, (hi - lo) // P, 2, P, 2], BF16) for c, (lo, hi) in enumerate(Z_CHUNKS)]
+        totals = [psum.tile([P, H], F32, name="total%d" % n) for n in range(V // P)]
+        z_rows = [sbuf("z_rows%d" % n, [P, 2, P, 2], BF16) for n in range(V // P)]
 
-        def gather_terms(b, lo, hi):
-            terms = []
+
+        def first_hop(b, lo, hi):
+            if lo > 0:
+                shared = sbuf("late_terms%d" % b, [P, D, hi - lo], F32, "term_%d_%d" % (BLOCKS - 1, b - 1))
             for d in range(D):
-                term = sbuf("term_%d_%d_%d" % (b, lo, d), [P, hi - lo], F32)
-                nc.vector.tensor_tensor(term[:], h[b][:].indirect(entries(pos_sb[d], lo, hi)), gate_rows[d][:, lo:hi], MULT)
-                terms.append(term)
-            return terms
-
-        def sum_and_turn(b, terms, lo, hi):
-            total = psum.tile([P, (hi - lo) // P, P], F32, name="total", tag="total", bufs=3)
-            for n in range((hi - lo) // P):
-                for d in range(D):
+                term = shared[:, d, :] if lo > 0 else sbuf("term_%d_%d" % (b, d), [P, hi - lo], F32)[:]
+                nc.vector.tensor_tensor(term, h[b][:].indirect(entries(pos_sb[d], lo, hi)), gate_rows[d][:, lo:hi], MULT)
+                for n in range(lo // P, hi // P):
                     nc.tensor.matmul(
-                        total[:, n, :], terms[d][:, n * P : (n + 1) * P], identity[:],
+                        totals[n][:, b * P : (b + 1) * P], term[:, n * P - lo : (n + 1) * P - lo], identity[:],
                         start=(d == 0), stop=(d == D - 1), is_transpose=True,
                     )
-            for c, (c_lo, c_hi) in enumerate(Z_CHUNKS):
-                if lo <= c_lo and c_hi <= hi:
-                    part = total[:, (c_lo - lo) // P : (c_hi - lo) // P, :]
-                    nc.scalar.copy(
-                        out=z_rows[c][:, :, :, 32 * b : 32 * (b + 1), :],
-                        in_=part.rearrange("v n (m u e) -> v n u m e", u=2, e=2),
-                    )
+
+        def round_z(n, first, last):
+            nc.scalar.copy(
+                out=z_rows[n][:, :, first // PACK : last // PACK, :],
+                in_=totals[n][:, first:last].rearrange("v (q u e) -> v u q e", u=2, e=2),
+            )
 
         g = sbuf("g", [P, V], F32)
 
-        def second_layer(c):
-            lo, hi = Z_CHUNKS[c]
+        def turn_z(lo, hi):
             tiles = (hi - lo) // P
-            pairs = z_rows[c][:].rearrange("v n u q e -> v (n u q e)").bitcast(F32)
-            turned = psum.tile([P, tiles, 2, P], F32, name="turned", tag="turned", bufs=2)
+            turned = psum.tile([P, tiles, 2, P], F32, name="turned", tag="product", bufs=4)
             for n in range(tiles):
+                pairs = z_rows[lo // P + n][:].rearrange("v u q e -> v (u q e)").bitcast(F32)
                 for u in range(2):
-                    nc.tensor.transpose(turned[:, n, u, :], pairs[:, (2 * n + u) * P : (2 * n + u + 1) * P], identity[:])
-            z_bf16 = sbuf("z_bf16_%d" % c, [P, PACK * (hi - lo)], BF16)
+                    nc.tensor.transpose(turned[:, n, u, :], pairs[:, u * P : (u + 1) * P], identity[:])
+            z_bf16 = sbuf("z_bf16_%d" % lo, [P, PACK * (hi - lo)], BF16)
             nc.scalar.copy(
                 out=z_bf16[:].bitcast(F32).rearrange("q (n v u) -> q n v u", n=tiles, u=2),
                 in_=turned[:].rearrange("q n u v -> q n v u"),
             )
-            z_codes = sbuf("z_codes%d" % c, [P, hi - lo], U32)
-            z_plane = sbuf("z_plane%d" % c, [P, hi - lo], U8)
-            nc.vector.quantize_mx(out=z_codes[:].bitcast(FP8X4), scales=z_plane[:], in_=z_bf16[:])
-            acc = psum.tile([P, hi - lo], F32, name="product", tag="product", bufs=3)
+            return z_bf16
+
+        def second_layer(lo, hi, z_bf16):
+            nc.vector.quantize_mx(out=z_codes[:, lo:hi].bitcast(FP8X4), scales=z_plane[:, lo:hi], in_=z_bf16[:])
+            acc = psum.tile([P, hi - lo], F32, name="product", tag="product", bufs=4)
             nc.tensor.matmul_mx(
                 out=acc[:],
                 lhsT=w2_codes[:].bitcast(FP4X4),
                 lhsT_scale=w2_plane[:],
-                rhs=z_codes[:].bitcast(FP8X4),
-                rhs_scale=z_plane[:],
+                rhs=z_codes[:, lo:hi].bitcast(FP8X4),
+                rhs_scale=z_plane[:, lo:hi],
                 start=True,
                 stop=True,
             )
             nc.scalar.activation(g[:, lo:hi], acc[:], RELU)
 
-        for b in range(BLOCKS - 1):
+        last = BLOCKS - 1
+        for b in range(1, BLOCKS):
+            if b > 1:
+                round_w1(b, nc.scalar.copy)
+                quantize_w1(b)
             for lo in range(0, S, 512):
-                first_layer(b + 1, lo, lo + 512)
-            if b + 2 < BLOCKS:
-                round_w1(b + 2, nc.scalar.copy)
-                quantize_w1(b + 2)
-            sum_and_turn(b, gather_terms(b, 0, V), 0, V)
-        for c, (lo, hi) in enumerate(Z_CHUNKS):
-            sum_and_turn(BLOCKS - 1, gather_terms(BLOCKS - 1, lo, hi), lo, hi)
-            second_layer(c)
+                first_layer(b, lo, lo + 512)
+            if b == 1:
+                first_hop(0, 0, V)
+        turned_z = []
+        for lo, hi, passes in ((0, 384, ((0, 256), (256, 384))), (384, V, ((384, V),))):
+            for b in range(1, BLOCKS):
+                first_hop(b, lo, hi)
+                if b >= last - 1:
+                    for n in range(lo // P, hi // P):
+                        round_z(n, 0 if b < last else last * P, (b + 1) * P)
+            for pass_lo, pass_hi in passes:
+                turned_z.append((pass_lo, pass_hi, turn_z(pass_lo, pass_hi)))
+        z_codes = sbuf("z_codes", [P, V], U32, "h%d" % last)
+        z_plane = sbuf("z_plane", [P, V], U8)
+        for lo, hi, z_bf16 in turned_z:
+            second_layer(lo, hi, z_bf16)
 
         roots = [sbuf("root_term%d" % d, [P, U], F32) for d in range(D)]
         for d in range(D):

@@ -60,17 +60,13 @@ def tile_picked_hop2_gelu_p_kernel(
         w2_codes = sbuf("w2_codes", [P, 2 * N], U8)
         w2_plane = sbuf("w2_plane", [P, N], U8)
         identity = sbuf("identity", [P, P], F32)
-        warm_in = sbuf("warm_in", [P, 8], F32)
-        warm_out = sbuf("warm_out", [P, 8], F32)
 
         nc.vector.memset(x_scale_table[:].bitcast(I32), 0)
-        nc.vector.memset(warm_in[:], 0.0)
         w1_rows = w1.rearrange("(p j) c -> p j c", j=PACK)
         nc.sync.dma_start(offs_sb[:], offs)
         nc.sync.dma_start(out=w1_first[:], in_=w1_rows[:, :, 0:P])
         load_scale_rows((nc.sync, nc.scalar), x_scale_table, x_scales[0])
         nc.sync.dma_start(out=x_table[:], in_=x_words[0].rearrange("p n t -> p (n t)").bitcast(I32))
-        nc.scalar.activation(warm_out[:], warm_in[:], GELU)
         nc.sync.dma_start(out=w1_rest[:], in_=w1_rows[:, :, P:H])
         nc.sync.dma_start(out=gate_first[:], in_=gate[0])
         nc.sync.dma_start(pos_sb[0][:], pos1)
@@ -88,23 +84,25 @@ def tile_picked_hop2_gelu_p_kernel(
 
         w1_bf16 = {}
         w1_codes = {}
-        w1_plane = [sbuf("w1_plane%d" % b, [P, P], U8) for b in range(BLOCKS)]
+        w1_plane = sbuf("w1_plane", [P, H], U8)
 
-        def round_w1(b, copy):
-            w1_bf16[b] = sbuf("w1_bf16_%d" % b, [P, P, PACK], BF16, "after_words" if b > 0 else None)
-            raw = w1_first[:] if b == 0 else w1_rest[:, :, (b - 1) * P : b * P]
+        def round_w1(first, last, copy):
+            raw = w1_first[:] if first == 0 else w1_rest[:, :, (first - 1) * P : (last - 1) * P]
+            w1_bf16[first] = sbuf("w1_bf16_%d" % first, [P, raw.shape[2], PACK], BF16, "after_words" if first > 0 else None)
             copy(
-                out=w1_bf16[b][:].rearrange("p (c i) j -> p c j i", i=4),
+                out=w1_bf16[first][:].rearrange("p (c i) j -> p c j i", i=4),
                 in_=raw.rearrange("p j (c i) -> p c j i", i=4),
             )
 
-        def quantize_w1(b):
-            w1_codes[b] = sbuf("w1_codes%d" % b, [P, P], U32, "after_scales" if b == 0 else None)
+        def quantize_w1(first, last):
+            codes = sbuf("w1_codes%d" % first, [P, (last - first) * P], U32, "after_scales" if first == 0 else None)
             nc.vector.quantize_mx(
-                out=w1_codes[b][:].bitcast(FP8X4),
-                scales=w1_plane[b][:],
-                in_=w1_bf16[b][:].rearrange("p c j -> p (c j)"),
+                out=codes[:].bitcast(FP8X4),
+                scales=w1_plane[:, first * P : last * P],
+                in_=w1_bf16[first][:].rearrange("p c j -> p (c j)"),
             )
+            for b in range(first, last):
+                w1_codes[b] = codes[:, (b - first) * P : (b - first + 1) * P]
 
         picked_plane = sbuf("picked_plane", [P, S], U8)
         picked_codes = sbuf("picked_codes", [P, S], U32)
@@ -114,8 +112,8 @@ def tile_picked_hop2_gelu_p_kernel(
             acc = psum.tile([P, hi - lo], F32, name="product", tag="product", bufs=4)
             nc.tensor.matmul_mx(
                 out=acc[:],
-                lhsT=w1_codes[b][:].bitcast(FP8X4),
-                lhsT_scale=w1_plane[b][:],
+                lhsT=w1_codes[b].bitcast(FP8X4),
+                lhsT_scale=w1_plane[:, b * P : (b + 1) * P],
                 rhs=picked_codes[:, lo:hi].bitcast(FP8X4),
                 rhs_scale=picked_plane[:, lo:hi],
                 start=True,
@@ -124,23 +122,21 @@ def tile_picked_hop2_gelu_p_kernel(
             nc.scalar.activation(h[b][:, lo:hi], acc[:], GELU)
 
         nc.vector.tensor_copy(picked_plane[:], x_scale_table[:].indirect(offs_sb[:]))
-        round_w1(0, nc.scalar.copy)
-        quantize_w1(0)
+        round_w1(0, 1, nc.scalar.copy)
+        quantize_w1(0, 1)
         for lo, hi in PICK_PIECES:
             nc.vector.tensor_copy(picked_codes[:, lo:hi], x_table[:].bitcast(U32).indirect(entries(offs_sb, lo, hi)))
             first_layer(0, lo, hi)
-        round_w1(1, nc.vector.tensor_copy)
-        quantize_w1(1)
+        round_w1(1, 2, nc.vector.tensor_copy)
+        quantize_w1(1, 2)
 
         totals = [psum.tile([P, H], F32, name="total%d" % n) for n in range(V // P)]
         z_rows = [sbuf("z_rows%d" % n, [P, 2, P, 2], BF16) for n in range(V // P)]
 
 
         def first_hop(b, lo, hi):
-            if lo > 0:
-                shared = sbuf("late_terms%d" % b, [P, D, hi - lo], F32, "term_%d_%d" % (BLOCKS - 1, b - 1))
             for d in range(D):
-                term = shared[:, d, :] if lo > 0 else sbuf("term_%d_%d" % (b, d), [P, hi - lo], F32)[:]
+                term = sbuf("term_%d_%d_%d" % (b, d, lo), [P, hi - lo], F32)[:]
                 nc.vector.tensor_tensor(term, h[b][:].indirect(entries(pos_sb[d], lo, hi)), gate_rows[d][:, lo:hi], MULT)
                 for n in range(lo // P, hi // P):
                     nc.tensor.matmul(
@@ -185,23 +181,22 @@ def tile_picked_hop2_gelu_p_kernel(
             nc.scalar.activation(g[:, lo:hi], acc[:], RELU)
 
         last = BLOCKS - 1
-        for b in range(1, BLOCKS):
-            if b > 1:
-                round_w1(b, nc.scalar.copy)
-                quantize_w1(b)
+        for b in range(last):
             for lo in range(0, S, 512):
-                first_layer(b, lo, lo + 512)
-            if b == 1:
-                first_hop(0, 0, V)
+                first_layer(b + 1, lo, lo + 512)
+            if b == 0:
+                round_w1(2, BLOCKS, nc.scalar.copy)
+                quantize_w1(2, BLOCKS)
+            first_hop(b, 0, V)
+            if b > 0:
+                for n in range(V // P):
+                    round_z(n, 0 if b == 1 else b * P, (b + 1) * P)
         turned_z = []
-        for lo, hi, passes in ((0, 384, ((0, 256), (256, 384))), (384, V, ((384, V),))):
-            for b in range(1, BLOCKS):
-                first_hop(b, lo, hi)
-                if b >= last - 1:
-                    for n in range(lo // P, hi // P):
-                        round_z(n, 0 if b < last else last * P, (b + 1) * P)
-            for pass_lo, pass_hi in passes:
-                turned_z.append((pass_lo, pass_hi, turn_z(pass_lo, pass_hi)))
+        for lo, hi in Z_CHUNKS:
+            first_hop(last, lo, hi)
+            for n in range(lo // P, hi // P):
+                round_z(n, last * P, H)
+            turned_z.append((lo, hi, turn_z(lo, hi)))
         z_codes = sbuf("z_codes", [P, V], U32, "h%d" % last)
         z_plane = sbuf("z_plane", [P, V], U8)
         for lo, hi, z_bf16 in turned_z:

@@ -32,8 +32,8 @@ def entries(list_tile, lo, hi):
 
 
 def load_scale_rows(queues, plane, rows):
-    for q in range(4):
-        queues[q % len(queues)].dma_start(out=plane[32 * q : 32 * q + 4, :].bitcast(I32), in_=rows[4 * q : 4 * q + 4, :].bitcast(I32))
+    for r in range(4):
+        queues[r % len(queues)].dma_start(out=plane[r:P:32, :].bitcast(I32), in_=rows[r:16:4, :].bitcast(I32))
 
 
 def tile_picked_hop2_gelu_p_kernel(
@@ -51,43 +51,48 @@ def tile_picked_hop2_gelu_p_kernel(
         pos_sb = [sbuf("pos_sb%d" % d, [P, V // LIST_ROWS], U16) for d in range(D)]
         nxt_sb = [sbuf("nxt_sb%d" % d, [P, U // LIST_ROWS], U16) for d in range(D)]
         x_table = sbuf("x_table", [P, T], I32, "after_words")
-        x_scale_table = sbuf("x_scale_table", [P, T], U8, "after_scales")
-        w1_first = sbuf("w1_first", [P, PACK, P], F32)
-        w1_rest = sbuf("w1_rest", [P, PACK, H - P], F32)
-        gate_first = sbuf("gate_first", [P, V], F32)
-        gate_rest = sbuf("gate_rest", [P, D - 1, V], F32)
+        x_scale_table = sbuf("x_scale_table", [P, T], U8)
+        w1_raw = {
+            0: sbuf("w1_raw0", [P, PACK, P], F32, "after_round0"),
+            1: sbuf("w1_raw1", [P, PACK, P], F32),
+            2: sbuf("w1_raw2", [P, PACK, 2 * P], F32, "after_round2"),
+        }
+        gate_sb = [sbuf("gate_sb%d" % d, [P, V], F32) for d in range(D)]
         gate2_sb = sbuf("gate2_sb", [P, D, U], F32)
         w2_codes = sbuf("w2_codes", [P, 2 * N], U8)
         w2_plane = sbuf("w2_plane", [P, N], U8)
         identity = sbuf("identity", [P, P], F32)
 
         nc.vector.memset(x_scale_table[:].bitcast(I32), 0)
+        nc.vector.memset(identity[:], 0.0)
+        nc.vector.memset(w2_plane[:].bitcast(I32), 0)
+        make_identity(nc, identity[:], nomemset=True)
         w1_rows = w1.rearrange("(p j) c -> p j c", j=PACK)
         nc.sync.dma_start(offs_sb[:], offs)
-        nc.sync.dma_start(out=w1_first[:], in_=w1_rows[:, :, 0:P])
+        nc.sync.dma_start(pos_sb[0][:], pos1)
         load_scale_rows((nc.sync, nc.scalar), x_scale_table, x_scales[0])
         nc.sync.dma_start(out=x_table[:], in_=x_words[0].rearrange("p n t -> p (n t)").bitcast(I32))
-        nc.sync.dma_start(out=w1_rest[:], in_=w1_rows[:, :, P:H])
-        nc.sync.dma_start(out=gate_first[:], in_=gate[0])
-        nc.sync.dma_start(pos_sb[0][:], pos1)
-        nc.sync.dma_start(out=gate_rest[:], in_=gate[1:D].rearrange("d p v -> p d v"))
+        nc.sync.dma_start(out=w1_raw[0][:], in_=w1_rows[:, :, 0:P])
+        nc.sync.dma_start(out=w1_raw[1][:], in_=w1_rows[:, :, P : 2 * P])
+        nc.sync.dma_start(out=gate_sb[0][:], in_=gate[0])
+        nc.sync.dma_start(out=gate_sb[1][:], in_=gate[1])
         nc.sync.dma_start(pos_sb[1][:], pos2)
+        nc.sync.dma_start(out=w1_raw[2][:], in_=w1_rows[:, :, 2 * P : H])
+        nc.sync.dma_start(out=gate_sb[2][:], in_=gate[2])
         nc.sync.dma_start(pos_sb[2][:], pos3)
-        make_identity(nc, identity[:])
-        nc.gpsimd.memset(w2_plane[:], 0)
         nc.sync.dma_start(out=w2_codes[:].bitcast(I32), in_=w2_words[0].bitcast(I32))
         load_scale_rows((nc.sync,), w2_plane, w2_scales[0])
         nc.sync.dma_start(out=gate2_sb[:], in_=gate2.rearrange("d p u -> p d u"))
         for tile, source in zip(nxt_sb, (nxt1, nxt2, nxt3)):
             nc.sync.dma_start(tile[:], source)
-        gate_rows = [gate_first[:]] + [gate_rest[:, d, :] for d in range(D - 1)]
+        gate_rows = [tile[:] for tile in gate_sb]
 
         w1_bf16 = {}
         w1_codes = {}
         w1_plane = sbuf("w1_plane", [P, H], U8)
 
         def round_w1(first, last, copy):
-            raw = w1_first[:] if first == 0 else w1_rest[:, :, (first - 1) * P : (last - 1) * P]
+            raw = w1_raw[first][:]
             w1_bf16[first] = sbuf("w1_bf16_%d" % first, [P, raw.shape[2], PACK], BF16, "after_words" if first > 0 else None)
             copy(
                 out=w1_bf16[first][:].rearrange("p (c i) j -> p c j i", i=4),
@@ -95,7 +100,7 @@ def tile_picked_hop2_gelu_p_kernel(
             )
 
         def quantize_w1(first, last):
-            codes = sbuf("w1_codes%d" % first, [P, (last - first) * P], U32, "after_scales" if first == 0 else None)
+            codes = sbuf("w1_codes%d" % first, [P, (last - first) * P], U32)
             nc.vector.quantize_mx(
                 out=codes[:].bitcast(FP8X4),
                 scales=w1_plane[:, first * P : last * P],
@@ -105,7 +110,7 @@ def tile_picked_hop2_gelu_p_kernel(
                 w1_codes[b] = codes[:, (b - first) * P : (b - first + 1) * P]
 
         picked_plane = sbuf("picked_plane", [P, S], U8)
-        picked_codes = sbuf("picked_codes", [P, S], U32)
+        picked_codes = {}
         h = [sbuf("h%d" % b, [P, S], F32) for b in range(BLOCKS)]
 
         def first_layer(b, lo, hi):
@@ -114,7 +119,7 @@ def tile_picked_hop2_gelu_p_kernel(
                 out=acc[:],
                 lhsT=w1_codes[b].bitcast(FP8X4),
                 lhsT_scale=w1_plane[:, b * P : (b + 1) * P],
-                rhs=picked_codes[:, lo:hi].bitcast(FP8X4),
+                rhs=picked_codes[lo // 512][:, lo % 512 : lo % 512 + hi - lo].bitcast(FP8X4),
                 rhs_scale=picked_plane[:, lo:hi],
                 start=True,
                 stop=True,
@@ -122,10 +127,16 @@ def tile_picked_hop2_gelu_p_kernel(
             nc.scalar.activation(h[b][:, lo:hi], acc[:], GELU)
 
         nc.vector.tensor_copy(picked_plane[:], x_scale_table[:].indirect(offs_sb[:]))
-        round_w1(0, 1, nc.scalar.copy)
-        quantize_w1(0, 1)
         for lo, hi in PICK_PIECES:
-            nc.vector.tensor_copy(picked_codes[:, lo:hi], x_table[:].bitcast(U32).indirect(entries(offs_sb, lo, hi)))
+            half = lo // 512
+            if half not in picked_codes:
+                picked_codes[half] = sbuf("picked_codes%d" % half, [P, 512], U32, "after_round0" if half else None)
+            nc.vector.tensor_copy(
+                picked_codes[half][:, lo % 512 : lo % 512 + hi - lo], x_table[:].bitcast(U32).indirect(entries(offs_sb, lo, hi))
+            )
+            if lo == 0:
+                round_w1(0, 1, nc.scalar.copy)
+                quantize_w1(0, 1)
             first_layer(0, lo, hi)
         round_w1(1, 2, nc.vector.tensor_copy)
         quantize_w1(1, 2)
@@ -136,7 +147,7 @@ def tile_picked_hop2_gelu_p_kernel(
 
         def first_hop(b, lo, hi):
             for d in range(D):
-                term = sbuf("term_%d_%d_%d" % (b, d, lo), [P, hi - lo], F32)[:]
+                term = sbuf("term_%d_%d_%d" % (b, d, lo), [P, hi - lo], F32, "after_round2" if (b, d) == (1, 0) else None)[:]
                 nc.vector.tensor_tensor(term, h[b][:].indirect(entries(pos_sb[d], lo, hi)), gate_rows[d][:, lo:hi], MULT)
                 for n in range(lo // P, hi // P):
                     nc.tensor.matmul(
@@ -184,10 +195,10 @@ def tile_picked_hop2_gelu_p_kernel(
         for b in range(last):
             for lo in range(0, S, 512):
                 first_layer(b + 1, lo, lo + 512)
+            first_hop(b, 0, V)
             if b == 0:
                 round_w1(2, BLOCKS, nc.scalar.copy)
                 quantize_w1(2, BLOCKS)
-            first_hop(b, 0, V)
             if b > 0:
                 for n in range(V // P):
                     round_z(n, 0 if b == 1 else b * P, (b + 1) * P)

@@ -24,7 +24,8 @@ PACK = 4
 LIST_ROWS = 16
 BLOCKS = H // P
 PICK_PIECES = ((0, 512), (512, 768), (768, 1024))
-Z_CHUNKS = ((0, 256), (256, 384), (384, 512))
+Z_CHUNKS = ((0, 256), (256, 384))
+LATE = 384
 
 
 def entries(list_tile, lo, hi):
@@ -52,11 +53,12 @@ def tile_picked_hop2_gelu_p_kernel(
         nxt_sb = [sbuf("nxt_sb%d" % d, [P, U // LIST_ROWS], U16) for d in range(D)]
         x_table = sbuf("x_table", [P, T], I32, "after_words")
         x_scale_table = sbuf("x_scale_table", [P, T], U8)
-        w1_raw = {
-            0: sbuf("w1_raw0", [P, PACK, P], F32, "after_round0"),
-            1: sbuf("w1_raw1", [P, PACK, P], F32),
-            2: sbuf("w1_raw2", [P, PACK, 2 * P], F32, "after_round2"),
-        }
+        w1_raw = [
+            sbuf("w1_raw0", [P, PACK, P], F32),
+            sbuf("w1_raw1", [P, PACK, P], F32, "after_round0"),
+            sbuf("w1_raw2", [P, PACK, 2 * P], F32),
+        ]
+        w1_raw1_again = sbuf("w1_raw1_again", [P, PACK, P], F32, "after_round2")
         gate_sb = [sbuf("gate_sb%d" % d, [P, V], F32) for d in range(D)]
         gate2_sb = sbuf("gate2_sb", [P, D, U], F32)
         w2_codes = sbuf("w2_codes", [P, 2 * N], U8)
@@ -74,10 +76,11 @@ def tile_picked_hop2_gelu_p_kernel(
         nc.sync.dma_start(out=x_table[:], in_=x_words[0].rearrange("p n t -> p (n t)").bitcast(I32))
         nc.sync.dma_start(out=w1_raw[0][:], in_=w1_rows[:, :, 0:P])
         nc.sync.dma_start(out=w1_raw[1][:], in_=w1_rows[:, :, P : 2 * P])
+        nc.sync.dma_start(out=w1_raw[2][:], in_=w1_rows[:, :, 2 * P : H])
         nc.sync.dma_start(out=gate_sb[0][:], in_=gate[0])
         nc.sync.dma_start(out=gate_sb[1][:], in_=gate[1])
         nc.sync.dma_start(pos_sb[1][:], pos2)
-        nc.sync.dma_start(out=w1_raw[2][:], in_=w1_rows[:, :, 2 * P : H])
+        nc.sync.dma_start(out=w1_raw1_again[:], in_=w1_rows[:, :, P : 2 * P])
         nc.sync.dma_start(out=gate_sb[2][:], in_=gate[2])
         nc.sync.dma_start(pos_sb[2][:], pos3)
         nc.sync.dma_start(out=w2_codes[:].bitcast(I32), in_=w2_words[0].bitcast(I32))
@@ -91,12 +94,16 @@ def tile_picked_hop2_gelu_p_kernel(
         w1_codes = {}
         w1_plane = sbuf("w1_plane", [P, H], U8)
 
-        def round_w1(first, last, copy):
-            raw = w1_raw[first][:]
-            w1_bf16[first] = sbuf("w1_bf16_%d" % first, [P, raw.shape[2], PACK], BF16, "after_words" if first > 0 else None)
+        def round_low(copy, target, raw):
             copy(
-                out=w1_bf16[first][:].rearrange("p (c i) j -> p c j i", i=4),
-                in_=raw.rearrange("p j (c i) -> p c j i", i=4),
+                out=target.rearrange("p (q e) j -> p q j e", e=2),
+                in_=raw.rearrange("p j (q t) -> p q j t", t=PACK)[:, :, :, 0:2],
+            )
+
+        def round_high(target, raw):
+            nc.scalar.copy(
+                out=target.rearrange("p e q j -> p q j e"),
+                in_=raw.rearrange("p j (q t) -> p q j t", t=PACK)[:, :, :, 2:4],
             )
 
         def quantize_w1(first, last):
@@ -104,7 +111,7 @@ def tile_picked_hop2_gelu_p_kernel(
             nc.vector.quantize_mx(
                 out=codes[:].bitcast(FP8X4),
                 scales=w1_plane[:, first * P : last * P],
-                in_=w1_bf16[first][:].rearrange("p c j -> p (c j)"),
+                in_=w1_bf16[first][:],
             )
             for b in range(first, last):
                 w1_codes[b] = codes[:, (b - first) * P : (b - first + 1) * P]
@@ -135,19 +142,23 @@ def tile_picked_hop2_gelu_p_kernel(
                 picked_codes[half][:, lo % 512 : lo % 512 + hi - lo], x_table[:].bitcast(U32).indirect(entries(offs_sb, lo, hi))
             )
             if lo == 0:
-                round_w1(0, 1, nc.scalar.copy)
+                w1_bf16[0] = sbuf("w1_bf16_0", [P, P * PACK], BF16)
+                columns = w1_bf16[0][:].rearrange("p (c j) -> p c j", j=PACK)
+                round_low(nc.scalar.copy, columns[:, 0 : P // 2, :], w1_raw[0][:])
+                round_low(nc.scalar.copy, columns[:, P // 2 : P, :], w1_raw[1][:])
                 quantize_w1(0, 1)
             first_layer(0, lo, hi)
-        round_w1(1, 2, nc.vector.tensor_copy)
+        w1_bf16[1] = sbuf("w1_bf16_1", [P, P * PACK], BF16, "after_words")
+        round_low(nc.vector.tensor_copy, w1_bf16[1][:].rearrange("p (c j) -> p c j", j=PACK), w1_raw[2][:])
         quantize_w1(1, 2)
 
         totals = [psum.tile([P, H], F32, name="total%d" % n) for n in range(V // P)]
-        z_rows = [sbuf("z_rows%d" % n, [P, 2, P, 2], BF16) for n in range(V // P)]
-
+        z_rows = [sbuf("z_rows%d" % n, [P, 2, P, 2], BF16, "late2" if n == 1 else None) for n in range(V // P)]
+        ties = {(1, 0, 0): "after_round2", (3, 0, 256): "late0", (3, 1, 256): "late1"}
 
         def first_hop(b, lo, hi):
             for d in range(D):
-                term = sbuf("term_%d_%d_%d" % (b, d, lo), [P, hi - lo], F32, "after_round2" if (b, d) == (1, 0) else None)[:]
+                term = sbuf("term_%d_%d_%d" % (b, d, lo), [P, hi - lo], F32, ties.get((b, d, lo)))[:]
                 nc.vector.tensor_tensor(term, h[b][:].indirect(entries(pos_sb[d], lo, hi)), gate_rows[d][:, lo:hi], MULT)
                 for n in range(lo // P, hi // P):
                     nc.tensor.matmul(
@@ -155,10 +166,11 @@ def tile_picked_hop2_gelu_p_kernel(
                         start=(d == 0), stop=(d == D - 1), is_transpose=True,
                     )
 
-        def round_z(n, first, last):
+        def round_z(n, u):
+            sums = totals[n][:, 2 * u * P : 2 * (u + 1) * P]
             nc.scalar.copy(
-                out=z_rows[n][:, :, first // PACK : last // PACK, :],
-                in_=totals[n][:, first:last].rearrange("v (q u e) -> v u q e", u=2, e=2),
+                out=z_rows[n][:, u, :, :],
+                in_=sums.rearrange("v (q e) -> v q e", e=2) if u == 0 else sums.rearrange("v (e q) -> v q e", e=2),
             )
 
         g = sbuf("g", [P, V], F32)
@@ -191,27 +203,53 @@ def tile_picked_hop2_gelu_p_kernel(
             )
             nc.scalar.activation(g[:, lo:hi], acc[:], RELU)
 
-        last = BLOCKS - 1
-        for b in range(last):
-            for lo in range(0, S, 512):
-                first_layer(b + 1, lo, lo + 512)
-            first_hop(b, 0, V)
-            if b == 0:
-                round_w1(2, BLOCKS, nc.scalar.copy)
-                quantize_w1(2, BLOCKS)
-            if b > 0:
-                for n in range(V // P):
-                    round_z(n, 0 if b == 1 else b * P, (b + 1) * P)
+        for lo in range(0, S, 512):
+            first_layer(1, lo, lo + 512)
+        first_hop(0, 0, V)
+        w1_bf16[2] = sbuf("w1_bf16_2", [P, 2 * P * PACK], BF16, "after_words")
+        columns = w1_bf16[2][:].rearrange("p (e q j) -> p e q j", e=2, j=PACK)
+        round_high(columns[:, :, 0:32, :], w1_raw[0][:])
+        round_high(columns[:, :, 64:128, :], w1_raw[2][:])
+        round_high(columns[:, :, 32:64, :], w1_raw1_again[:])
+        quantize_w1(2, BLOCKS)
+        for lo in range(0, S, 512):
+            first_layer(2, lo, lo + 512)
+        first_hop(1, 0, V)
+        for lo in range(0, S, 512):
+            first_layer(3, lo, lo + 512)
+        for n in range(V // P):
+            round_z(n, 0)
+        z_late = sbuf("z_late", [P, PACK * (V - LATE)], BF16)
+        turned_late = psum.tile([P, P], F32, name="turned_late", tag="product", bufs=4)
+        nc.tensor.transpose(turned_late[:], z_rows[LATE // P][:, 0, :, :].rearrange("v q e -> v (q e)").bitcast(F32), identity[:])
+        nc.scalar.copy(out=z_late[:].bitcast(F32).rearrange("q (v u) -> q v u", u=2)[:, :, 0], in_=turned_late[:])
+        first_hop(2, 0, LATE)
         turned_z = []
         for lo, hi in Z_CHUNKS:
-            first_hop(last, lo, hi)
+            first_hop(3, lo, hi)
             for n in range(lo // P, hi // P):
-                round_z(n, last * P, H)
+                round_z(n, 1)
             turned_z.append((lo, hi, turn_z(lo, hi)))
-        z_codes = sbuf("z_codes", [P, V], U32, "h%d" % last)
+        late_terms = [sbuf("late_term%d" % d, [P, 2, V - LATE], F32, "late%d" % d) for d in range(D)]
+        late_partial = sbuf("late_partial", [P, 2, V - LATE], F32)
+        for d in range(D):
+            for e in range(2):
+                nc.vector.tensor_tensor(
+                    late_terms[d][:, e, :], h[2 + e][:].indirect(entries(pos_sb[d], LATE, V)), gate_rows[d][:, LATE:V], MULT
+                )
+                if (d, e) == (D - 1, 0):
+                    nc.vector.tensor_tensor(late_partial[:], late_terms[0][:], late_terms[1][:], ADD)
+        z_codes = sbuf("z_codes", [P, V], U32, "h2")
         z_plane = sbuf("z_plane", [P, V], U8)
-        for lo, hi, z_bf16 in turned_z:
-            second_layer(lo, hi, z_bf16)
+        second_layer(*turned_z[0])
+        nc.vector.tensor_tensor(
+            z_late[:].rearrange("q (v u e) -> q v u e", u=2, e=2)[:, :, 1, :],
+            late_partial[:].rearrange("q e v -> q v e"),
+            late_terms[D - 1][:].rearrange("q e v -> q v e"),
+            ADD,
+        )
+        second_layer(*turned_z[1])
+        second_layer(LATE, V, z_late)
 
         roots = [sbuf("root_term%d" % d, [P, U], F32) for d in range(D)]
         for d in range(D):

@@ -72,9 +72,9 @@ def tile_picked_hop2_gelu_p_kernel(
         w1_rows = w1.rearrange("(p j) c -> p j c", j=PACK)
         nc.sync.dma_start(offs_sb[:], offs)
         nc.sync.dma_start(pos_sb[0][:], pos1)
-        load_scale_rows((nc.sync, nc.scalar), x_scale_table, x_scales[0])
+        nc.scalar.dma_start(out=w1_raw[0][:], in_=w1_rows[:, :, 0:P])
+        load_scale_rows((nc.sync,), x_scale_table, x_scales[0])
         nc.sync.dma_start(out=x_table[:], in_=x_words[0].rearrange("p n t -> p (n t)").bitcast(I32))
-        nc.sync.dma_start(out=w1_raw[0][:], in_=w1_rows[:, :, 0:P])
         nc.sync.dma_start(out=w1_raw[1][:], in_=w1_rows[:, :, P : 2 * P])
         nc.sync.dma_start(out=w1_raw[2][:], in_=w1_rows[:, :, 2 * P : H])
         nc.sync.dma_start(out=gate_sb[0][:], in_=gate[0])

@@ -153,8 +153,8 @@ def tile_picked_hop2_gelu_p_kernel(
         quantize_w1(1, 2)
 
         totals = [psum.tile([P, H], F32, name="total%d" % n) for n in range(V // P)]
-        z_rows = [sbuf("z_rows%d" % n, [P, 2, P, 2], BF16, "late2" if n == 1 else None) for n in range(V // P)]
-        ties = {(1, 0, 0): "after_round2", (3, 0, 256): "late0", (3, 1, 256): "late1"}
+        z_rows = [sbuf("z_rows%d" % n, [P, 2, P, 2], BF16, "late_z" if n == 1 else None) for n in range(V // P)]
+        ties = {(1, 0, 0): "after_round2", (3, 2, 0): "late0", (3, 0, 256): "late1", (3, 1, 256): "late2"}
 
         def first_hop(b, lo, hi):
             for d in range(D):
@@ -219,10 +219,8 @@ def tile_picked_hop2_gelu_p_kernel(
             first_layer(3, lo, lo + 512)
         for n in range(V // P):
             round_z(n, 0)
-        z_late = sbuf("z_late", [P, PACK * (V - LATE)], BF16)
-        turned_late = psum.tile([P, P], F32, name="turned_late", tag="product", bufs=4)
-        nc.tensor.transpose(turned_late[:], z_rows[LATE // P][:, 0, :, :].rearrange("v q e -> v (q e)").bitcast(F32), identity[:])
-        nc.scalar.copy(out=z_late[:].bitcast(F32).rearrange("q (v u) -> q v u", u=2)[:, :, 0], in_=turned_late[:])
+        turned_late = psum.tile([P, P, 1], F32, name="turned_late", tag="product", bufs=4)
+        nc.tensor.transpose(turned_late[:, :, 0], z_rows[LATE // P][:, 0, :, :].rearrange("v q e -> v (q e)").bitcast(F32), identity[:])
         first_hop(2, 0, LATE)
         turned_z = []
         for lo, hi in Z_CHUNKS:
@@ -230,6 +228,9 @@ def tile_picked_hop2_gelu_p_kernel(
             for n in range(lo // P, hi // P):
                 round_z(n, 1)
             turned_z.append((lo, hi, turn_z(lo, hi)))
+            if lo == 0:
+                z_late = sbuf("z_late", [P, PACK * (V - LATE)], BF16, "late_z")
+                nc.scalar.copy(out=z_late[:].bitcast(F32).rearrange("q (v u) -> q v u", u=2), in_=turned_late[:].to_broadcast([P, P, 2]))
         late_terms = [sbuf("late_term%d" % d, [P, 2, V - LATE], F32, "late%d" % d) for d in range(D)]
         late_partial = sbuf("late_partial", [P, 2, V - LATE], F32)
         for d in range(D):

@@ -51,7 +51,7 @@ def tile_picked_hop2_gelu_p_kernel(
         offs_sb = sbuf("offs_sb", [P, S // LIST_ROWS], U16)
         pos_sb = [sbuf("pos_sb%d" % d, [P, V // LIST_ROWS], U16) for d in range(D)]
         nxt_sb = [sbuf("nxt_sb%d" % d, [P, U // LIST_ROWS], U16) for d in range(D)]
-        x_table = sbuf("x_table", [P, T], I32, "after_words")
+        x_table = sbuf("x_table", [P, T], I32)
         x_scale_table = sbuf("x_scale_table", [P, T], U8)
         w1_raw = [
             sbuf("w1_raw0", [P, PACK, P], F32),
@@ -148,7 +148,7 @@ def tile_picked_hop2_gelu_p_kernel(
                 round_low(nc.scalar.copy, columns[:, P // 2 : P, :], w1_raw[1][:])
                 quantize_w1(0, 1)
             first_layer(0, lo, hi)
-        w1_bf16[1] = sbuf("w1_bf16_1", [P, P * PACK], BF16, "after_words")
+        w1_bf16[1] = sbuf("w1_bf16_1", [P, P * PACK], BF16, "w1_bf16_0")
         round_low(nc.vector.tensor_copy, w1_bf16[1][:].rearrange("p (c j) -> p c j", j=PACK), w1_raw[2][:])
         quantize_w1(1, 2)
 
@@ -175,16 +175,15 @@ def tile_picked_hop2_gelu_p_kernel(
 
         g = sbuf("g", [P, V], F32)
 
-        def turn_z(lo, hi):
-            tiles = (hi - lo) // P
-            turned = psum.tile([P, tiles, 2, P], F32, name="turned", tag="product", bufs=4)
-            for n in range(tiles):
-                pairs = z_rows[lo // P + n][:].rearrange("v u q e -> v (u q e)").bitcast(F32)
-                for u in range(2):
-                    nc.tensor.transpose(turned[:, n, u, :], pairs[:, u * P : (u + 1) * P], identity[:])
+        def turn_z(turned, lo, hi, u):
+            for n in range((hi - lo) // P):
+                pairs = z_rows[lo // P + n][:, u, :, :].rearrange("v q e -> v (q e)").bitcast(F32)
+                nc.tensor.transpose(turned[:, n, u, :], pairs, identity[:])
+
+        def weave_z(turned, lo, hi):
             z_bf16 = sbuf("z_bf16_%d" % lo, [P, PACK * (hi - lo)], BF16)
             nc.scalar.copy(
-                out=z_bf16[:].bitcast(F32).rearrange("q (n v u) -> q n v u", n=tiles, u=2),
+                out=z_bf16[:].bitcast(F32).rearrange("q (n v u) -> q n v u", v=P, u=2),
                 in_=turned[:].rearrange("q n u v -> q n v u"),
             )
             return z_bf16
@@ -206,7 +205,7 @@ def tile_picked_hop2_gelu_p_kernel(
         for lo in range(0, S, 512):
             first_layer(1, lo, lo + 512)
         first_hop(0, 0, V)
-        w1_bf16[2] = sbuf("w1_bf16_2", [P, 2 * P * PACK], BF16, "after_words")
+        w1_bf16[2] = sbuf("w1_bf16_2", [P, 2 * P * PACK], BF16, "w1_bf16_0")
         columns = w1_bf16[2][:].rearrange("p (e q j) -> p e q j", e=2, j=PACK)
         round_high(columns[:, :, 0:32, :], w1_raw[0][:])
         round_high(columns[:, :, 64:128, :], w1_raw[2][:])
@@ -221,13 +220,18 @@ def tile_picked_hop2_gelu_p_kernel(
             round_z(n, 0)
         turned_late = psum.tile([P, P, 1], F32, name="turned_late", tag="product", bufs=4)
         nc.tensor.transpose(turned_late[:, :, 0], z_rows[LATE // P][:, 0, :, :].rearrange("v q e -> v (q e)").bitcast(F32), identity[:])
+        turned = {}
+        for lo, hi in Z_CHUNKS:
+            turned[lo] = psum.tile([P, (hi - lo) // P, 2, P], F32, name="turned%d" % lo, tag="product", bufs=4)
+            turn_z(turned[lo], lo, hi, 0)
         first_hop(2, 0, LATE)
         turned_z = []
         for lo, hi in Z_CHUNKS:
             first_hop(3, lo, hi)
             for n in range(lo // P, hi // P):
                 round_z(n, 1)
-            turned_z.append((lo, hi, turn_z(lo, hi)))
+            turn_z(turned[lo], lo, hi, 1)
+            turned_z.append((lo, hi, weave_z(turned[lo], lo, hi)))
             if lo == 0:
                 z_late = sbuf("z_late", [P, PACK * (V - LATE)], BF16, "late_z")
                 nc.scalar.copy(out=z_late[:].bitcast(F32).rearrange("q (v u) -> q v u", u=2), in_=turned_late[:].to_broadcast([P, P, 2]))

@@ -147,7 +147,9 @@ def tile_picked_hop2_gelu_p_kernel(
                 round_low(nc.scalar.copy, columns[:, 0 : P // 2, :], w1_raw[0][:])
                 round_low(nc.scalar.copy, columns[:, P // 2 : P, :], w1_raw[1][:])
                 quantize_w1(0, 1)
-            first_layer(0, lo, hi)
+            width = hi - lo if hi < S else P
+            for start in range(lo, hi, width):
+                first_layer(0, start, start + width)
         w1_bf16[1] = sbuf("w1_bf16_1", [P, P * PACK], BF16, "w1_bf16_0")
         round_low(nc.vector.tensor_copy, w1_bf16[1][:].rearrange("p (c j) -> p c j", j=PACK), w1_raw[2][:])
         quantize_w1(1, 2)
@@ -213,9 +215,9 @@ def tile_picked_hop2_gelu_p_kernel(
         quantize_w1(2, BLOCKS)
         for lo in range(0, S, 512):
             first_layer(2, lo, lo + 512)
-        first_hop(1, 0, V)
         for lo in range(0, S, 512):
             first_layer(3, lo, lo + 512)
+        first_hop(1, 0, V)
         for n in range(V // P):
             round_z(n, 0)
         turned_late = psum.tile([P, P, 1], F32, name="turned_late", tag="product", bufs=4)

@@ -24,8 +24,7 @@ PACK = 4
 LIST_ROWS = 16
 BLOCKS = H // P
 PICK_PIECES = ((0, 512), (512, 768), (768, 1024))
-Z_CHUNKS = ((0, 256), (256, 384))
-LATE = 384
+LATE = 256
 
 
 def entries(list_tile, lo, hi):
@@ -58,7 +57,6 @@ def tile_picked_hop2_gelu_p_kernel(
             sbuf("w1_raw1", [P, PACK, P], F32, "after_round0"),
             sbuf("w1_raw2", [P, PACK, 2 * P], F32),
         ]
-        w1_raw1_again = sbuf("w1_raw1_again", [P, PACK, P], F32, "after_round2")
         gate_sb = [sbuf("gate_sb%d" % d, [P, V], F32) for d in range(D)]
         gate2_sb = sbuf("gate2_sb", [P, D, U], F32)
         w2_codes = sbuf("w2_codes", [P, 2 * N], U8)
@@ -80,7 +78,6 @@ def tile_picked_hop2_gelu_p_kernel(
         nc.sync.dma_start(out=gate_sb[0][:], in_=gate[0])
         nc.sync.dma_start(out=gate_sb[1][:], in_=gate[1])
         nc.sync.dma_start(pos_sb[1][:], pos2)
-        nc.sync.dma_start(out=w1_raw1_again[:], in_=w1_rows[:, :, P : 2 * P])
         nc.sync.dma_start(out=gate_sb[2][:], in_=gate[2])
         nc.sync.dma_start(pos_sb[2][:], pos3)
         nc.sync.dma_start(out=w2_codes[:].bitcast(I32), in_=w2_words[0].bitcast(I32))
@@ -100,8 +97,8 @@ def tile_picked_hop2_gelu_p_kernel(
                 in_=raw.rearrange("p j (q t) -> p q j t", t=PACK)[:, :, :, 0:2],
             )
 
-        def round_high(target, raw):
-            nc.scalar.copy(
+        def round_high(copy, target, raw):
+            copy(
                 out=target.rearrange("p e q j -> p q j e"),
                 in_=raw.rearrange("p j (q t) -> p q j t", t=PACK)[:, :, :, 2:4],
             )
@@ -133,6 +130,8 @@ def tile_picked_hop2_gelu_p_kernel(
             )
             nc.scalar.activation(h[b][:, lo:hi], acc[:], GELU)
 
+        w1_bf16[2] = sbuf("w1_bf16_2", [P, 2 * P * PACK], BF16)
+        high_columns = w1_bf16[2][:].rearrange("p (e q j) -> p e q j", e=2, j=PACK)
         nc.vector.tensor_copy(picked_plane[:], x_scale_table[:].indirect(offs_sb[:]))
         for lo, hi in PICK_PIECES:
             half = lo // 512
@@ -144,29 +143,44 @@ def tile_picked_hop2_gelu_p_kernel(
             if lo == 0:
                 w1_bf16[0] = sbuf("w1_bf16_0", [P, P * PACK], BF16)
                 columns = w1_bf16[0][:].rearrange("p (c j) -> p c j", j=PACK)
+                warm = sbuf("warm", [P, 1], F32)
+                nc.scalar.activation(warm[:], w1_raw[0][:, 0, 0:1], GELU)
                 round_low(nc.scalar.copy, columns[:, 0 : P // 2, :], w1_raw[0][:])
+                round_high(nc.scalar.copy, high_columns[:, :, 0:32, :], w1_raw[0][:])
                 round_low(nc.scalar.copy, columns[:, P // 2 : P, :], w1_raw[1][:])
+                round_high(nc.scalar.copy, high_columns[:, :, 32:64, :], w1_raw[1][:])
                 quantize_w1(0, 1)
             width = hi - lo if hi < S else P
             for start in range(lo, hi, width):
                 first_layer(0, start, start + width)
         w1_bf16[1] = sbuf("w1_bf16_1", [P, P * PACK], BF16, "w1_bf16_0")
+        round_high(nc.vector.tensor_copy, high_columns[:, :, 64:128, :], w1_raw[2][:])
         round_low(nc.vector.tensor_copy, w1_bf16[1][:].rearrange("p (c j) -> p c j", j=PACK), w1_raw[2][:])
+        quantize_w1(2, BLOCKS)
         quantize_w1(1, 2)
 
         totals = [psum.tile([P, H], F32, name="total%d" % n) for n in range(V // P)]
-        z_rows = [sbuf("z_rows%d" % n, [P, 2, P, 2], BF16, "late_z" if n == 1 else None) for n in range(V // P)]
-        ties = {(1, 0, 0): "after_round2", (3, 2, 0): "late0", (3, 0, 256): "late1", (3, 1, 256): "late2"}
+        z_rows = [sbuf("z_rows%d" % n, [P, 2, P, 2], BF16) for n in range(V // P)]
+        z_bf16 = [sbuf("z_bf16_%d" % n, [P, PACK * P], BF16) for n in range(V // P)]
+        g = sbuf("g", [P, V], F32)
+        z_codes = sbuf("z_codes", [P, V], U32)
+        z_plane = sbuf("z_plane", [P, V], U8)
+        early_tiles = range(LATE // P)
+        late_tiles = range(LATE // P, V // P)
 
-        def first_hop(b, lo, hi):
-            for d in range(D):
-                term = sbuf("term_%d_%d_%d" % (b, d, lo), [P, hi - lo], F32, ties.get((b, d, lo)))[:]
-                nc.vector.tensor_tensor(term, h[b][:].indirect(entries(pos_sb[d], lo, hi)), gate_rows[d][:, lo:hi], MULT)
-                for n in range(lo // P, hi // P):
-                    nc.tensor.matmul(
-                        totals[n][:, b * P : (b + 1) * P], term[:, n * P - lo : (n + 1) * P - lo], identity[:],
-                        start=(d == 0), stop=(d == D - 1), is_transpose=True,
-                    )
+        def gated_term(b, d, lo, hi):
+            term = sbuf("term_%d_%d_%d" % (b, d, lo), [P, hi - lo], F32)
+            nc.vector.tensor_tensor(term[:], h[b][:].indirect(entries(pos_sb[d], lo, hi)), gate_rows[d][:, lo:hi], MULT)
+            return term
+
+        def turned_term(b, d, lo, hi):
+            term = gated_term(b, d, lo, hi)
+            for n in reversed(range(lo // P, hi // P)):
+                last = D - 2 if b >= 2 and n in late_tiles else D - 1
+                nc.tensor.matmul(
+                    totals[n][:, b * P : (b + 1) * P], term[:, n * P - lo : (n + 1) * P - lo], identity[:],
+                    start=(d == 0), stop=(d == last), is_transpose=True,
+                )
 
         def round_z(n, u):
             sums = totals[n][:, 2 * u * P : 2 * (u + 1) * P]
@@ -175,88 +189,74 @@ def tile_picked_hop2_gelu_p_kernel(
                 in_=sums.rearrange("v (q e) -> v q e", e=2) if u == 0 else sums.rearrange("v (e q) -> v q e", e=2),
             )
 
-        g = sbuf("g", [P, V], F32)
+        def turn_z(target, n, u):
+            nc.tensor.transpose(target, z_rows[n][:, u, :, :].rearrange("v q e -> v (q e)").bitcast(F32), identity[:])
 
-        def turn_z(turned, lo, hi, u):
-            for n in range((hi - lo) // P):
-                pairs = z_rows[lo // P + n][:, u, :, :].rearrange("v q e -> v (q e)").bitcast(F32)
-                nc.tensor.transpose(turned[:, n, u, :], pairs, identity[:])
-
-        def weave_z(turned, lo, hi):
-            z_bf16 = sbuf("z_bf16_%d" % lo, [P, PACK * (hi - lo)], BF16)
-            nc.scalar.copy(
-                out=z_bf16[:].bitcast(F32).rearrange("q (n v u) -> q n v u", v=P, u=2),
-                in_=turned[:].rearrange("q n u v -> q n v u"),
-            )
-            return z_bf16
-
-        def second_layer(lo, hi, z_bf16):
-            nc.vector.quantize_mx(out=z_codes[:, lo:hi].bitcast(FP8X4), scales=z_plane[:, lo:hi], in_=z_bf16[:])
-            acc = psum.tile([P, hi - lo], F32, name="product", tag="product", bufs=4)
+        def second_layer(n):
+            cols = slice(n * P, (n + 1) * P)
+            nc.vector.quantize_mx(out=z_codes[:, cols].bitcast(FP8X4), scales=z_plane[:, cols], in_=z_bf16[n][:])
+            acc = psum.tile([P, P], F32, name="second%d" % n, tag="total%d" % n)
             nc.tensor.matmul_mx(
                 out=acc[:],
                 lhsT=w2_codes[:].bitcast(FP4X4),
                 lhsT_scale=w2_plane[:],
-                rhs=z_codes[:, lo:hi].bitcast(FP8X4),
-                rhs_scale=z_plane[:, lo:hi],
+                rhs=z_codes[:, cols].bitcast(FP8X4),
+                rhs_scale=z_plane[:, cols],
                 start=True,
                 stop=True,
             )
-            nc.scalar.activation(g[:, lo:hi], acc[:], RELU)
+            nc.scalar.activation(g[:, cols], acc[:], RELU)
 
         for lo in range(0, S, 512):
             first_layer(1, lo, lo + 512)
-        first_hop(0, 0, V)
-        w1_bf16[2] = sbuf("w1_bf16_2", [P, 2 * P * PACK], BF16, "w1_bf16_0")
-        columns = w1_bf16[2][:].rearrange("p (e q j) -> p e q j", e=2, j=PACK)
-        round_high(columns[:, :, 0:32, :], w1_raw[0][:])
-        round_high(columns[:, :, 64:128, :], w1_raw[2][:])
-        round_high(columns[:, :, 32:64, :], w1_raw1_again[:])
-        quantize_w1(2, BLOCKS)
-        for lo in range(0, S, 512):
-            first_layer(2, lo, lo + 512)
-        for lo in range(0, S, 512):
-            first_layer(3, lo, lo + 512)
-        first_hop(1, 0, V)
+        for d in range(D):
+            turned_term(0, d, 0, V)
+        for b in (2, 3):
+            for lo in range(0, S, 512):
+                first_layer(b, lo, lo + 512)
+        for d in range(D):
+            turned_term(1, d, 0, V)
         for n in range(V // P):
             round_z(n, 0)
-        turned_late = psum.tile([P, P, 1], F32, name="turned_late", tag="product", bufs=4)
-        nc.tensor.transpose(turned_late[:, :, 0], z_rows[LATE // P][:, 0, :, :].rearrange("v q e -> v (q e)").bitcast(F32), identity[:])
-        turned = {}
-        for lo, hi in Z_CHUNKS:
-            turned[lo] = psum.tile([P, (hi - lo) // P, 2, P], F32, name="turned%d" % lo, tag="product", bufs=4)
-            turn_z(turned[lo], lo, hi, 0)
-        first_hop(2, 0, LATE)
-        turned_z = []
-        for lo, hi in Z_CHUNKS:
-            first_hop(3, lo, hi)
-            for n in range(lo // P, hi // P):
-                round_z(n, 1)
-            turn_z(turned[lo], lo, hi, 1)
-            turned_z.append((lo, hi, weave_z(turned[lo], lo, hi)))
-            if lo == 0:
-                z_late = sbuf("z_late", [P, PACK * (V - LATE)], BF16, "late_z")
-                nc.scalar.copy(out=z_late[:].bitcast(F32).rearrange("q (v u) -> q v u", u=2), in_=turned_late[:].to_broadcast([P, P, 2]))
-        late_terms = [sbuf("late_term%d" % d, [P, 2, V - LATE], F32, "late%d" % d) for d in range(D)]
-        late_partial = sbuf("late_partial", [P, 2, V - LATE], F32)
-        for d in range(D):
+        turned_low = psum.tile([P, len(late_tiles), P], F32, name="turned_low", tag="product", bufs=4)
+        for i, n in enumerate(late_tiles):
+            turn_z(turned_low[:, i, :], n, 0)
+        for i, n in enumerate(late_tiles):
+            nc.scalar.copy(out=z_bf16[n][:].bitcast(F32).rearrange("q (v u) -> q v u", u=2)[:, :, 0], in_=turned_low[:, i, :])
+        turned = [psum.tile([P, 2, P], F32, name="turned%d" % n, tag="product", bufs=4) for n in early_tiles]
+        for n in early_tiles:
+            turn_z(turned[n][:, 0, :], n, 0)
+        partial_back = psum.tile([P, len(late_tiles), 2, P], F32, name="partial_back", tag="product", bufs=4)
+        for e in range(2):
+            for d in range(D - 1):
+                turned_term(2 + e, d, 0, V)
+            for i, n in enumerate(late_tiles):
+                rows = sbuf("partial_rows%d_%d" % (n, e), [P, P], F32)
+                nc.scalar.copy(out=rows[:], in_=totals[n][:, (2 + e) * P : (3 + e) * P])
+                nc.tensor.transpose(partial_back[:, i, e, :], rows[:], identity[:])
+            turned_term(2 + e, D - 1, 0, LATE)
+        for n in early_tiles:
+            round_z(n, 1)
+        for n in early_tiles:
+            turn_z(turned[n][:, 1, :], n, 1)
+        for n in early_tiles:
+            nc.scalar.copy(out=z_bf16[n][:].bitcast(F32).rearrange("q (v u) -> q v u", u=2), in_=turned[n][:].rearrange("q u v -> q v u"))
+        last_terms = {n: sbuf("last_terms%d" % n, [P, 2, P], F32) for n in late_tiles}
+        for n in late_tiles:
+            lo, hi = n * P, (n + 1) * P
             for e in range(2):
                 nc.vector.tensor_tensor(
-                    late_terms[d][:, e, :], h[2 + e][:].indirect(entries(pos_sb[d], LATE, V)), gate_rows[d][:, LATE:V], MULT
+                    last_terms[n][:, e, :], h[2 + e][:].indirect(entries(pos_sb[D - 1], lo, hi)), gate_rows[D - 1][:, lo:hi], MULT
                 )
-                if (d, e) == (D - 1, 0):
-                    nc.vector.tensor_tensor(late_partial[:], late_terms[0][:], late_terms[1][:], ADD)
-        z_codes = sbuf("z_codes", [P, V], U32, "h2")
-        z_plane = sbuf("z_plane", [P, V], U8)
-        second_layer(*turned_z[0])
-        nc.vector.tensor_tensor(
-            z_late[:].rearrange("q (v u e) -> q v u e", u=2, e=2)[:, :, 1, :],
-            late_partial[:].rearrange("q e v -> q v e"),
-            late_terms[D - 1][:].rearrange("q e v -> q v e"),
-            ADD,
-        )
-        second_layer(*turned_z[1])
-        second_layer(LATE, V, z_late)
+        for n in late_tiles:
+            nc.vector.tensor_tensor(
+                z_bf16[n][:].rearrange("q (v u e) -> q v u e", u=2, e=2)[:, :, 1, :],
+                last_terms[n][:].rearrange("q e v -> q v e"),
+                partial_back[:, n - LATE // P, :, :].rearrange("q e v -> q v e"),
+                ADD,
+            )
+        for n in list(late_tiles) + list(early_tiles):
+            second_layer(n)
 
         roots = [sbuf("root_term%d" % d, [P, U], F32) for d in range(D)]
         for d in range(D):

@@ -54,9 +54,10 @@ def tile_picked_hop2_gelu_p_kernel(
         x_scale_table = sbuf("x_scale_table", [P, T], U8)
         w1_raw = [
             sbuf("w1_raw0", [P, PACK, P], F32),
-            sbuf("w1_raw1", [P, PACK, P], F32, "after_round0"),
+            sbuf("w1_raw1", [P, 2, P], F32, "after_round0"),
             sbuf("w1_raw2", [P, PACK, 2 * P], F32),
         ]
+        w1_raw1_first = sbuf("w1_raw1_first", [P, 2, P], F32)
         gate_sb = [sbuf("gate_sb%d" % d, [P, V], F32) for d in range(D)]
         gate2_sb = sbuf("gate2_sb", [P, D, U], F32)
         w2_codes = sbuf("w2_codes", [P, 2 * N], U8)
@@ -73,7 +74,8 @@ def tile_picked_hop2_gelu_p_kernel(
         nc.scalar.dma_start(out=w1_raw[0][:], in_=w1_rows[:, :, 0:P])
         load_scale_rows((nc.sync,), x_scale_table, x_scales[0])
         nc.sync.dma_start(out=x_table[:], in_=x_words[0].rearrange("p n t -> p (n t)").bitcast(I32))
-        nc.sync.dma_start(out=w1_raw[1][:], in_=w1_rows[:, :, P : 2 * P])
+        nc.sync.dma_start(out=w1_raw1_first[:], in_=w1_rows[:, 0:2, P : 2 * P])
+        nc.sync.dma_start(out=w1_raw[1][:], in_=w1_rows[:, 2:4, P : 2 * P])
         nc.sync.dma_start(out=w1_raw[2][:], in_=w1_rows[:, :, 2 * P : H])
         nc.sync.dma_start(out=gate_sb[0][:], in_=gate[0])
         nc.sync.dma_start(out=gate_sb[1][:], in_=gate[1])
@@ -147,8 +149,10 @@ def tile_picked_hop2_gelu_p_kernel(
                 nc.scalar.activation(warm[:], w1_raw[0][:, 0, 0:1], GELU)
                 round_low(nc.scalar.copy, columns[:, 0 : P // 2, :], w1_raw[0][:])
                 round_high(nc.scalar.copy, high_columns[:, :, 0:32, :], w1_raw[0][:])
-                round_low(nc.scalar.copy, columns[:, P // 2 : P, :], w1_raw[1][:])
-                round_high(nc.scalar.copy, high_columns[:, :, 32:64, :], w1_raw[1][:])
+                round_low(nc.scalar.copy, columns[:, P // 2 : P, 0:2], w1_raw1_first[:])
+                round_high(nc.scalar.copy, high_columns[:, :, 32:64, 0:2], w1_raw1_first[:])
+                round_low(nc.scalar.copy, columns[:, P // 2 : P, 2:4], w1_raw[1][:])
+                round_high(nc.scalar.copy, high_columns[:, :, 32:64, 2:4], w1_raw[1][:])
                 quantize_w1(0, 1)
             width = hi - lo if hi < S else P
             for start in range(lo, hi, width):

@@ -55,7 +55,8 @@ def tile_picked_hop2_gelu_p_kernel(
         w1_raw = [
             sbuf("w1_raw0", [P, PACK, P], F32),
             sbuf("w1_raw1", [P, 2, P], F32, "after_round0"),
-            sbuf("w1_raw2", [P, PACK, 2 * P], F32),
+            sbuf("w1_raw2", [P, PACK, P], F32),
+            sbuf("w1_raw3", [P, PACK, P], F32),
         ]
         w1_raw1_first = sbuf("w1_raw1_first", [P, 2, P], F32)
         gate_sb = [sbuf("gate_sb%d" % d, [P, V], F32) for d in range(D)]
@@ -76,7 +77,8 @@ def tile_picked_hop2_gelu_p_kernel(
         nc.sync.dma_start(out=x_table[:], in_=x_words[0].rearrange("p n t -> p (n t)").bitcast(I32))
         nc.sync.dma_start(out=w1_raw1_first[:], in_=w1_rows[:, 0:2, P : 2 * P])
         nc.sync.dma_start(out=w1_raw[1][:], in_=w1_rows[:, 2:4, P : 2 * P])
-        nc.sync.dma_start(out=w1_raw[2][:], in_=w1_rows[:, :, 2 * P : H])
+        nc.sync.dma_start(out=w1_raw[2][:], in_=w1_rows[:, :, 2 * P : 3 * P])
+        nc.sync.dma_start(out=w1_raw[3][:], in_=w1_rows[:, :, 3 * P : H])
         nc.sync.dma_start(out=gate_sb[0][:], in_=gate[0])
         nc.sync.dma_start(out=gate_sb[1][:], in_=gate[1])
         nc.sync.dma_start(pos_sb[1][:], pos2)
@@ -154,12 +156,15 @@ def tile_picked_hop2_gelu_p_kernel(
                 round_low(nc.scalar.copy, columns[:, P // 2 : P, 2:4], w1_raw[1][:])
                 round_high(nc.scalar.copy, high_columns[:, :, 32:64, 2:4], w1_raw[1][:])
                 quantize_w1(0, 1)
-            width = hi - lo if hi < S else P
+                w1_bf16[1] = sbuf("w1_bf16_1", [P, P * PACK], BF16)
+                low_columns = w1_bf16[1][:].rearrange("p (c j) -> p c j", j=PACK)
+                round_high(nc.scalar.copy, high_columns[:, :, 64:96, :], w1_raw[2][:])
+                round_low(nc.scalar.copy, low_columns[:, 0:64, :], w1_raw[2][:])
+            width = 2 * P if hi < S else P
             for start in range(lo, hi, width):
                 first_layer(0, start, start + width)
-        w1_bf16[1] = sbuf("w1_bf16_1", [P, P * PACK], BF16, "w1_bf16_0")
-        round_high(nc.vector.tensor_copy, high_columns[:, :, 64:128, :], w1_raw[2][:])
-        round_low(nc.vector.tensor_copy, w1_bf16[1][:].rearrange("p (c j) -> p c j", j=PACK), w1_raw[2][:])
+        round_high(nc.vector.tensor_copy, high_columns[:, :, 96:128, :], w1_raw[3][:])
+        round_low(nc.vector.tensor_copy, low_columns[:, 64:128, :], w1_raw[3][:])
         quantize_w1(2, BLOCKS)
         quantize_w1(1, 2)
 

@@ -85,7 +85,11 @@ def tile_picked_hop2_gelu_p_kernel(
         nc.sync.dma_start(out=gate_sb[2][:], in_=gate[2])
         nc.sync.dma_start(pos_sb[2][:], pos3)
         nc.sync.dma_start(out=w2_codes[:].bitcast(I32), in_=w2_words[0].bitcast(I32))
-        load_scale_rows((nc.sync,), w2_plane, w2_scales[0])
+        for r in range(4):
+            for q in range(2):
+                nc.sync.dma_start(
+                    out=w2_plane[32 * q + r : P : 64, :].bitcast(I32), in_=w2_scales[0][4 * q + r : 16 : 8, :].bitcast(I32)
+                )
         nc.sync.dma_start(out=gate2_sb[:], in_=gate2.rearrange("d p u -> p d u"))
         for tile, source in zip(nxt_sb, (nxt1, nxt2, nxt3)):
             nc.sync.dma_start(tile[:], source)

@@ -18,6 +18,7 @@ MULT = mybir.AluOpType.mult
 ADD = mybir.AluOpType.add
 GELU = mybir.ActivationFunctionType.Gelu_apprx_tanh
 RELU = mybir.ActivationFunctionType.Relu
+COPY = mybir.ActivationFunctionType.Copy
 
 P = 128
 PACK = 4
@@ -172,8 +173,11 @@ def tile_picked_hop2_gelu_p_kernel(
         quantize_w1(2, BLOCKS)
         quantize_w1(1, 2)
 
-        totals = [psum.tile([P, H], F32, name="total%d" % n) for n in range(V // P)]
-        z_rows = [sbuf("z_rows%d" % n, [P, 2, P, 2], BF16) for n in range(V // P)]
+        low_sums = [psum.tile([P, V // P, P], F32, name="low_sums%d" % b, tag="total%d" % b) for b in range(2)]
+        early_sums = psum.tile([P, LATE // P, 2, P], F32, name="early_sums", tag="total2")
+        late_sums = psum.tile([P, (V - LATE) // P, 2, P], F32, name="late_sums", tag="total3")
+        low_rows = sbuf("low_rows", [P, V // P, 2, P], BF16)
+        high_rows = sbuf("high_rows", [P, LATE // P, P, 2], BF16)
         z_bf16 = [sbuf("z_bf16_%d" % n, [P, PACK * P], BF16) for n in range(V // P)]
         g = sbuf("g", [P, V], F32)
         z_codes = sbuf("z_codes", [P, V], U32)
@@ -181,29 +185,41 @@ def tile_picked_hop2_gelu_p_kernel(
         early_tiles = range(LATE // P)
         late_tiles = range(LATE // P, V // P)
 
+        fetched = {}
+
+        def fetch(b, d):
+            fetched[b, d] = sbuf("fetched_%d_%d" % (b, d), [P, V], F32)
+            nc.scalar.activation(fetched[b, d][:], h[b][:].indirect(pos_sb[d][:]), COPY)
+
         def gated_term(b, d, lo, hi):
-            term = sbuf("term_%d_%d_%d" % (b, d, lo), [P, hi - lo], F32)
-            nc.vector.tensor_tensor(term[:], h[b][:].indirect(entries(pos_sb[d], lo, hi)), gate_rows[d][:, lo:hi], MULT)
+            term = keep.tile([P, hi - lo], F32, name="term_%d_%d_%d" % (b, d, lo), tag="term", bufs=3, align_bytes=64)
+            if (b, d) in fetched:
+                nc.vector.tensor_tensor(term[:], fetched[b, d][:, lo:hi], gate_rows[d][:, lo:hi], MULT)
+            else:
+                nc.vector.tensor_tensor(term[:], h[b][:].indirect(entries(pos_sb[d], lo, hi)), gate_rows[d][:, lo:hi], MULT)
             return term
 
         def turned_term(b, d, lo, hi):
             term = gated_term(b, d, lo, hi)
-            for n in reversed(range(lo // P, hi // P)):
-                last = D - 2 if b >= 2 and n in late_tiles else D - 1
+            for n in sorted(range(lo // P, hi // P), key=lambda n: (b >= 2 and n in early_tiles, n)):
+                if b < 2:
+                    target = low_sums[b][:, n, :]
+                    first, last = (d, n) == (0, 0), (d, n) == (D - 1, V // P - 1)
+                elif n in early_tiles:
+                    target = early_sums[:, n, b - 2, :]
+                    first, last = (b, d, n) == (2, 1, 0), (b, d, n) == (3, D - 1, LATE // P - 1)
+                else:
+                    target = late_sums[:, n - LATE // P, b - 2, :]
+                    first, last = (b, d, n) == (2, 1, LATE // P), (b, d, n) == (3, D - 2, V // P - 1)
                 nc.tensor.matmul(
-                    totals[n][:, b * P : (b + 1) * P], term[:, n * P - lo : (n + 1) * P - lo], identity[:],
-                    start=(d == 0), stop=(d == last), is_transpose=True,
+                    target, term[:, n * P - lo : (n + 1) * P - lo], identity[:], start=first, stop=last, is_transpose=True
                 )
 
-        def round_z(n, u):
-            sums = totals[n][:, 2 * u * P : 2 * (u + 1) * P]
-            nc.scalar.copy(
-                out=z_rows[n][:, u, :, :],
-                in_=sums.rearrange("v (q e) -> v q e", e=2) if u == 0 else sums.rearrange("v (e q) -> v q e", e=2),
-            )
+        def round_low_sums(b):
+            nc.scalar.copy(out=low_rows[:, :, b, :], in_=low_sums[b][:])
 
-        def turn_z(target, n, u):
-            nc.tensor.transpose(target, z_rows[n][:, u, :, :].rearrange("v q e -> v (q e)").bitcast(F32), identity[:])
+        def turn_low(target, n):
+            nc.tensor.transpose(target, low_rows[:, n, :, :].rearrange("v b c -> v (b c)").bitcast(F32), identity[:])
 
         def second_layer(n):
             cols = slice(n * P, (n + 1) * P)
@@ -227,34 +243,42 @@ def tile_picked_hop2_gelu_p_kernel(
         for b in (2, 3):
             for lo in range(0, S, 512):
                 first_layer(b, lo, lo + 512)
+        fetch(1, 2)
+        round_low_sums(0)
+        fetch(2, 0)
+        fetch(3, 0)
+        fetch(3, 1)
         for d in range(D):
             turned_term(1, d, 0, V)
-        for n in range(V // P):
-            round_z(n, 0)
+        round_low_sums(1)
         turned_low = psum.tile([P, len(late_tiles), P], F32, name="turned_low", tag="product", bufs=4)
         for i, n in enumerate(late_tiles):
-            turn_z(turned_low[:, i, :], n, 0)
+            turn_low(turned_low[:, i, :], n)
         for i, n in enumerate(late_tiles):
             nc.scalar.copy(out=z_bf16[n][:].bitcast(F32).rearrange("q (v u) -> q v u", u=2)[:, :, 0], in_=turned_low[:, i, :])
         turned = [psum.tile([P, 2, P], F32, name="turned%d" % n, tag="product", bufs=4) for n in early_tiles]
         for n in early_tiles:
-            turn_z(turned[n][:, 0, :], n, 0)
+            turn_low(turned[n][:, 0, :], n)
         partial_back = psum.tile([P, len(late_tiles), 2, P], F32, name="partial_back", tag="product", bufs=4)
-        for e in range(2):
-            for d in range(D - 1):
-                turned_term(2 + e, d, 0, V)
-            for i, n in enumerate(late_tiles):
-                rows = sbuf("partial_rows%d_%d" % (n, e), [P, P], F32)
-                nc.scalar.copy(out=rows[:], in_=totals[n][:, (2 + e) * P : (3 + e) * P])
-                nc.tensor.transpose(partial_back[:, i, e, :], rows[:], identity[:])
-            turned_term(2 + e, D - 1, 0, LATE)
+        turned_term(2, 1, 0, V)
+        turned_term(2, 0, 0, V)
+        turned_term(3, 0, 0, V)
+        turned_term(2, 2, 0, LATE)
+        turned_term(3, 1, 0, V)
+        partial_rows = [sbuf("partial_rows%d" % n, [P, 2, P], F32) for n in late_tiles]
+        for i in range(len(late_tiles)):
+            nc.scalar.copy(out=partial_rows[i][:], in_=late_sums[:, i, :, :])
+        for i in range(len(late_tiles)):
+            for plane in range(2):
+                nc.tensor.transpose(partial_back[:, i, plane, :], partial_rows[i][:, plane, :], identity[:])
+        turned_term(3, 2, 0, LATE)
         for n in early_tiles:
-            round_z(n, 1)
+            nc.scalar.copy(out=high_rows[:, n, :, :], in_=early_sums[:, n, :, :].rearrange("v e q -> v q e"))
         for n in early_tiles:
-            turn_z(turned[n][:, 1, :], n, 1)
+            nc.tensor.transpose(turned[n][:, 1, :], high_rows[:, n, :, :].rearrange("v q e -> v (q e)").bitcast(F32), identity[:])
         for n in early_tiles:
             nc.scalar.copy(out=z_bf16[n][:].bitcast(F32).rearrange("q (v u) -> q v u", u=2), in_=turned[n][:].rearrange("q u v -> q v u"))
-        last_terms = {n: sbuf("last_terms%d" % n, [P, 2, P], F32) for n in late_tiles}
+        last_terms = {n: keep.tile([P, 2, P], F32, name="last_terms%d" % n, tag="term", bufs=3, align_bytes=64) for n in late_tiles}
         for n in late_tiles:
             lo, hi = n * P, (n + 1) * P
             for e in range(2):

@@ -176,7 +176,6 @@ def tile_picked_hop2_gelu_p_kernel(
         low_sums = [psum.tile([P, V // P, P], F32, name="low_sums%d" % b, tag="total%d" % b) for b in range(2)]
         early_sums = psum.tile([P, LATE // P, 2, P], F32, name="early_sums", tag="total2")
         late_sums = psum.tile([P, (V - LATE) // P, 2, P], F32, name="late_sums", tag="total3")
-        low_rows = sbuf("low_rows", [P, V // P, 2, P], BF16)
         high_rows = sbuf("high_rows", [P, LATE // P, P, 2], BF16)
         z_bf16 = [sbuf("z_bf16_%d" % n, [P, PACK * P], BF16) for n in range(V // P)]
         g = sbuf("g", [P, V], F32)
@@ -244,13 +243,22 @@ def tile_picked_hop2_gelu_p_kernel(
             for lo in range(0, S, 512):
                 first_layer(b, lo, lo + 512)
         fetch(1, 2)
-        round_low_sums(0)
         fetch(2, 0)
         fetch(3, 0)
         fetch(3, 1)
         for d in range(D):
             turned_term(1, d, 0, V)
+        turned_term(2, 1, 0, V)
+        turned_term(2, 0, 0, V)
+        low_rows = sbuf("low_rows", [P, V // P, 2, P], BF16, "fetched_2_0")
+        round_low_sums(0)
         round_low_sums(1)
+        turned_term(3, 0, 0, V)
+        partial_back = psum.tile([P, len(late_tiles), 2, P], F32, name="partial_back", tag="product", bufs=4)
+        turned_term(3, 1, 0, V)
+        partial_rows = [sbuf("partial_rows%d" % n, [P, 2, P], F32) for n in late_tiles]
+        for i in range(len(late_tiles)):
+            nc.scalar.copy(out=partial_rows[i][:], in_=late_sums[:, i, :, :])
         turned_low = psum.tile([P, len(late_tiles), P], F32, name="turned_low", tag="product", bufs=4)
         for i, n in enumerate(late_tiles):
             turn_low(turned_low[:, i, :], n)
@@ -259,19 +267,11 @@ def tile_picked_hop2_gelu_p_kernel(
         turned = [psum.tile([P, 2, P], F32, name="turned%d" % n, tag="product", bufs=4) for n in early_tiles]
         for n in early_tiles:
             turn_low(turned[n][:, 0, :], n)
-        partial_back = psum.tile([P, len(late_tiles), 2, P], F32, name="partial_back", tag="product", bufs=4)
-        turned_term(2, 1, 0, V)
-        turned_term(2, 0, 0, V)
-        turned_term(3, 0, 0, V)
         turned_term(2, 2, 0, LATE)
-        turned_term(3, 1, 0, V)
-        partial_rows = [sbuf("partial_rows%d" % n, [P, 2, P], F32) for n in late_tiles]
-        for i in range(len(late_tiles)):
-            nc.scalar.copy(out=partial_rows[i][:], in_=late_sums[:, i, :, :])
+        turned_term(3, 2, 0, LATE)
         for i in range(len(late_tiles)):
             for plane in range(2):
                 nc.tensor.transpose(partial_back[:, i, plane, :], partial_rows[i][:, plane, :], identity[:])
-        turned_term(3, 2, 0, LATE)
         for n in early_tiles:
             nc.scalar.copy(out=high_rows[:, n, :, :], in_=early_sums[:, n, :, :].rearrange("v e q -> v q e"))
         for n in early_tiles:

from contextlib import ExitStack

import concourse.mybir as mybir
from concourse.masks import make_identity

K, T, S, D, V, H, N, U = 512, 2048, 1024, 3, 512, 512, 128, 256
FLOPS = 2 * K * H * S + 2 * H * N * V

F32 = mybir.dt.float32
BF16 = mybir.dt.bfloat16
I32 = mybir.dt.int32
U32 = mybir.dt.uint32
U16 = mybir.dt.uint16
U8 = mybir.dt.uint8
FP8X4 = mybir.dt.float8_e4m3fn_x4
FP4X4 = mybir.dt.float4_e2m1fn_x4
MULT = mybir.AluOpType.mult
ADD = mybir.AluOpType.add
GELU = mybir.ActivationFunctionType.Gelu_apprx_tanh
RELU = mybir.ActivationFunctionType.Relu
COPY = mybir.ActivationFunctionType.Copy

P = 128
PACK = 4
LIST_ROWS = 16
BLOCKS = H // P
PICK_PIECES = ((0, 512), (512, 768), (768, 1024))
LATE = 256


def entries(list_tile, lo, hi):
    return list_tile[:, lo // LIST_ROWS : hi // LIST_ROWS]


def load_scale_rows(queues, plane, rows):
    for r in range(4):
        queues[r % len(queues)].dma_start(out=plane[r:P:32, :].bitcast(I32), in_=rows[r:16:4, :].bitcast(I32))


def tile_picked_hop2_gelu_p_kernel(
    tc, x_words, x_scales, w1, w2_words, w2_scales, gate, gate2, offs, pos1, pos2, pos3, nxt1, nxt2, nxt3, out
):
    nc = tc.nc
    with ExitStack() as ctx:
        keep = ctx.enter_context(tc.tile_pool(name="keep", bufs=1))
        psum = ctx.enter_context(tc.psum_pool(name="psum", bufs=1))

        def sbuf(name, shape, dtype, tag=None):
            return keep.tile(shape, dtype, name=name, tag=tag or name, align_bytes=64)

        offs_sb = sbuf("offs_sb", [P, S // LIST_ROWS], U16)
        pos_sb = [sbuf("pos_sb%d" % d, [P, V // LIST_ROWS], U16) for d in range(D)]
        nxt_sb = [sbuf("nxt_sb%d" % d, [P, U // LIST_ROWS], U16) for d in range(D)]
        x_table = sbuf("x_table", [P, T], I32)
        x_scale_table = sbuf("x_scale_table", [P, T], U8)
        w1_raw = [
            sbuf("w1_raw0", [P, PACK, P], F32),
            sbuf("w1_raw1", [P, 2, P], F32, "after_round0"),
            sbuf("w1_raw2", [P, PACK, P], F32),
            sbuf("w1_raw3", [P, PACK, P], F32),
        ]
        w1_raw1_first = sbuf("w1_raw1_first", [P, 2, P], F32)
        gate_sb = [sbuf("gate_sb%d" % d, [P, V], F32) for d in range(D)]
        gate2_sb = sbuf("gate2_sb", [P, D, U], F32)
        w2_codes = sbuf("w2_codes", [P, 2 * N], U8)
        w2_plane = sbuf("w2_plane", [P, N], U8)
        identity = sbuf("identity", [P, P], F32)

        nc.vector.memset(x_scale_table[:].bitcast(I32), 0)
        nc.vector.memset(identity[:], 0.0)
        nc.vector.memset(w2_plane[:].bitcast(I32), 0)
        make_identity(nc, identity[:], nomemset=True)
        w1_rows = w1.rearrange("(p j) c -> p j c", j=PACK)
        nc.sync.dma_start(offs_sb[:], offs)
        nc.sync.dma_start(pos_sb[0][:], pos1)
        nc.scalar.dma_start(out=w1_raw[0][:], in_=w1_rows[:, :, 0:P])
        load_scale_rows((nc.sync,), x_scale_table, x_scales[0])
        nc.sync.dma_start(out=x_table[:], in_=x_words[0].rearrange("p n t -> p (n t)").bitcast(I32))
        nc.sync.dma_start(out=w1_raw1_first[:], in_=w1_rows[:, 0:2, P : 2 * P])
        nc.sync.dma_start(out=w1_raw[1][:], in_=w1_rows[:, 2:4, P : 2 * P])
        nc.sync.dma_start(out=w1_raw[2][:], in_=w1_rows[:, :, 2 * P : 3 * P])
        nc.sync.dma_start(out=w1_raw[3][:], in_=w1_rows[:, :, 3 * P : H])
        nc.sync.dma_start(out=gate_sb[0][:], in_=gate[0])
        nc.sync.dma_start(out=gate_sb[1][:], in_=gate[1])
        nc.sync.dma_start(pos_sb[1][:], pos2)
        nc.sync.dma_start(out=gate_sb[2][:], in_=gate[2])
        nc.sync.dma_start(pos_sb[2][:], pos3)
        nc.sync.dma_start(out=w2_codes[:].bitcast(I32), in_=w2_words[0].bitcast(I32))
        for r in range(4):
            for q in range(2):
                nc.sync.dma_start(
                    out=w2_plane[32 * q + r : P : 64, :].bitcast(I32), in_=w2_scales[0][4 * q + r : 16 : 8, :].bitcast(I32)
                )
        nc.sync.dma_start(out=gate2_sb[:], in_=gate2.rearrange("d p u -> p d u"))
        for tile, source in zip(nxt_sb, (nxt1, nxt2, nxt3)):
            nc.sync.dma_start(tile[:], source)
        gate_rows = [tile[:] for tile in gate_sb]

        w1_bf16 = {}
        w1_codes = {}
        w1_plane = sbuf("w1_plane", [P, H], U8)

        def round_low(copy, target, raw):
            copy(
                out=target.rearrange("p (q e) j -> p q j e", e=2),
                in_=raw.rearrange("p j (q t) -> p q j t", t=PACK)[:, :, :, 0:2],
            )

        def round_high(copy, target, raw):
            copy(
                out=target.rearrange("p e q j -> p q j e"),
                in_=raw.rearrange("p j (q t) -> p q j t", t=PACK)[:, :, :, 2:4],
            )

        def quantize_w1(first, last):
            codes = sbuf("w1_codes%d" % first, [P, (last - first) * P], U32)
            nc.vector.quantize_mx(
                out=codes[:].bitcast(FP8X4),
                scales=w1_plane[:, first * P : last * P],
                in_=w1_bf16[first][:],
            )
            for b in range(first, last):
                w1_codes[b] = codes[:, (b - first) * P : (b - first + 1) * P]

        picked_plane = sbuf("picked_plane", [P, S], U8)
        picked_codes = {}
        h = [sbuf("h%d" % b, [P, S], F32) for b in range(BLOCKS)]

        def first_layer(b, lo, hi):
            acc = psum.tile([P, hi - lo], F32, name="product", tag="product", bufs=4)
            nc.tensor.matmul_mx(
                out=acc[:],
                lhsT=w1_codes[b].bitcast(FP8X4),
                lhsT_scale=w1_plane[:, b * P : (b + 1) * P],
                rhs=picked_codes[lo // 512][:, lo % 512 : lo % 512 + hi - lo].bitcast(FP8X4),
                rhs_scale=picked_plane[:, lo:hi],
                start=True,
                stop=True,
            )
            nc.scalar.activation(h[b][:, lo:hi], acc[:], GELU)

        w1_bf16[2] = sbuf("w1_bf16_2", [P, 2 * P * PACK], BF16)
        high_columns = w1_bf16[2][:].rearrange("p (e q j) -> p e q j", e=2, j=PACK)
        nc.vector.tensor_copy(picked_plane[:], x_scale_table[:].indirect(offs_sb[:]))
        for lo, hi in PICK_PIECES:
            half = lo // 512
            if half not in picked_codes:
                picked_codes[half] = sbuf("picked_codes%d" % half, [P, 512], U32, "after_round0" if half else None)
            nc.vector.tensor_copy(
                picked_codes[half][:, lo % 512 : lo % 512 + hi - lo], x_table[:].bitcast(U32).indirect(entries(offs_sb, lo, hi))
            )
            if lo == 0:
                w1_bf16[0] = sbuf("w1_bf16_0", [P, P * PACK], BF16)
                columns = w1_bf16[0][:].rearrange("p (c j) -> p c j", j=PACK)
                warm = sbuf("warm", [P, 1], F32)
                nc.scalar.activation(warm[:], w1_raw[0][:, 0, 0:1], GELU)
                round_low(nc.scalar.copy, columns[:, 0 : P // 2, :], w1_raw[0][:])
                round_high(nc.scalar.copy, high_columns[:, :, 0:32, :], w1_raw[0][:])
                round_low(nc.scalar.copy, columns[:, P // 2 : P, 0:2], w1_raw1_first[:])
                round_high(nc.scalar.copy, high_columns[:, :, 32:64, 0:2], w1_raw1_first[:])
                round_low(nc.scalar.copy, columns[:, P // 2 : P, 2:4], w1_raw[1][:])
                round_high(nc.scalar.copy, high_columns[:, :, 32:64, 2:4], w1_raw[1][:])
                quantize_w1(0, 1)
                w1_bf16[1] = sbuf("w1_bf16_1", [P, P * PACK], BF16)
                low_columns = w1_bf16[1][:].rearrange("p (c j) -> p c j", j=PACK)
                round_high(nc.scalar.copy, high_columns[:, :, 64:96, :], w1_raw[2][:])
                round_low(nc.scalar.copy, low_columns[:, 0:64, :], w1_raw[2][:])
            width = 2 * P if hi < S else P
            for start in range(lo, hi, width):
                first_layer(0, start, start + width)
        round_high(nc.vector.tensor_copy, high_columns[:, :, 96:128, :], w1_raw[3][:])
        round_low(nc.vector.tensor_copy, low_columns[:, 64:128, :], w1_raw[3][:])
        quantize_w1(2, BLOCKS)
        quantize_w1(1, 2)

        low_sums = [psum.tile([P, V // P, P], F32, name="low_sums%d" % b, tag="total%d" % b) for b in range(2)]
        early_sums = psum.tile([P, LATE // P, 2, P], F32, name="early_sums", tag="total2")
        late_sums = psum.tile([P, (V - LATE) // P, 2, P], F32, name="late_sums", tag="total3")
        high_rows = sbuf("high_rows", [P, LATE // P, P, 2], BF16)
        z_bf16 = [sbuf("z_bf16_%d" % n, [P, PACK * P], BF16) for n in range(V // P)]
        g = sbuf("g", [P, V], F32)
        z_codes = sbuf("z_codes", [P, V], U32)
        z_plane = sbuf("z_plane", [P, V], U8)
        early_tiles = range(LATE // P)
        late_tiles = range(LATE // P, V // P)

        fetched = {}

        def fetch(b, d):
            fetched[b, d] = sbuf("fetched_%d_%d" % (b, d), [P, V], F32)
            nc.scalar.activation(fetched[b, d][:], h[b][:].indirect(pos_sb[d][:]), COPY)

        def gated_term(b, d, lo, hi):
            term = keep.tile([P, hi - lo], F32, name="term_%d_%d_%d" % (b, d, lo), tag="term", bufs=3, align_bytes=64)
            if (b, d) in fetched:
                nc.vector.tensor_tensor(term[:], fetched[b, d][:, lo:hi], gate_rows[d][:, lo:hi], MULT)
            else:
                nc.vector.tensor_tensor(term[:], h[b][:].indirect(entries(pos_sb[d], lo, hi)), gate_rows[d][:, lo:hi], MULT)
            return term

        def turned_term(b, d, lo, hi):
            term = gated_term(b, d, lo, hi)
            for n in sorted(range(lo // P, hi // P), key=lambda n: (b >= 2 and n in early_tiles, n)):
                if b < 2:
                    target = low_sums[b][:, n, :]
                    first, last = (d, n) == (0, 0), (d, n) == (D - 1, V // P - 1)
                elif n in early_tiles:
                    target = early_sums[:, n, b - 2, :]
                    first, last = (b, d, n) == (2, 1, 0), (b, d, n) == (3, D - 1, LATE // P - 1)
                else:
                    target = late_sums[:, n - LATE // P, b - 2, :]
                    first, last = (b, d, n) == (2, 1, LATE // P), (b, d, n) == (3, D - 2, V // P - 1)
                nc.tensor.matmul(
                    target, term[:, n * P - lo : (n + 1) * P - lo], identity[:], start=first, stop=last, is_transpose=True
                )

        def round_low_sums(b):
            nc.scalar.copy(out=low_rows[:, :, b, :], in_=low_sums[b][:])

        def turn_low(target, n):
            nc.tensor.transpose(target, low_rows[:, n, :, :].rearrange("v b c -> v (b c)").bitcast(F32), identity[:])

        def second_layer(n):
            cols = slice(n * P, (n + 1) * P)
            nc.vector.quantize_mx(out=z_codes[:, cols].bitcast(FP8X4), scales=z_plane[:, cols], in_=z_bf16[n][:])
            acc = psum.tile([P, P], F32, name="second%d" % n, tag="total%d" % n)
            nc.tensor.matmul_mx(
                out=acc[:],
                lhsT=w2_codes[:].bitcast(FP4X4),
                lhsT_scale=w2_plane[:],
                rhs=z_codes[:, cols].bitcast(FP8X4),
                rhs_scale=z_plane[:, cols],
                start=True,
                stop=True,
            )
            nc.scalar.activation(g[:, cols], acc[:], RELU)

        for lo in range(0, S, 512):
            first_layer(1, lo, lo + 512)
        for d in range(D):
            turned_term(0, d, 0, V)
        for b in (2, 3):
            for lo in range(0, S, 512):
                first_layer(b, lo, lo + 512)
        fetch(1, 2)
        fetch(2, 0)
        fetch(3, 0)
        fetch(3, 1)
        for d in range(D):
            turned_term(1, d, 0, V)
        turned_term(2, 1, 0, V)
        turned_term(2, 0, 0, V)
        low_rows = sbuf("low_rows", [P, V // P, 2, P], BF16, "fetched_2_0")
        round_low_sums(0)
        round_low_sums(1)
        turned_term(3, 0, 0, V)
        partial_back = psum.tile([P, len(late_tiles), 2, P], F32, name="partial_back", tag="product", bufs=4)
        turned_term(3, 1, 0, V)
        partial_rows = [sbuf("partial_rows%d" % n, [P, 2, P], F32) for n in late_tiles]
        for i in range(len(late_tiles)):
            nc.scalar.copy(out=partial_rows[i][:], in_=late_sums[:, i, :, :])
        turned_low = psum.tile([P, len(late_tiles), P], F32, name="turned_low", tag="product", bufs=4)
        for i, n in enumerate(late_tiles):
            turn_low(turned_low[:, i, :], n)
        for i, n in enumerate(late_tiles):
            nc.scalar.copy(out=z_bf16[n][:].bitcast(F32).rearrange("q (v u) -> q v u", u=2)[:, :, 0], in_=turned_low[:, i, :])
        turned = [psum.tile([P, 2, P], F32, name="turned%d" % n, tag="product", bufs=4) for n in early_tiles]
        for n in early_tiles:
            turn_low(turned[n][:, 0, :], n)
        turned_term(2, 2, 0, LATE)
        turned_term(3, 2, 0, LATE)
        for i in range(len(late_tiles)):
            for plane in range(2):
                nc.tensor.transpose(partial_back[:, i, plane, :], partial_rows[i][:, plane, :], identity[:])
        for n in early_tiles:
            nc.scalar.copy(out=high_rows[:, n, :, :], in_=early_sums[:, n, :, :].rearrange("v e q -> v q e"))
        for n in early_tiles:
            nc.tensor.transpose(turned[n][:, 1, :], high_rows[:, n, :, :].rearrange("v q e -> v (q e)").bitcast(F32), identity[:])
        for n in early_tiles:
            nc.scalar.copy(out=z_bf16[n][:].bitcast(F32).rearrange("q (v u) -> q v u", u=2), in_=turned[n][:].rearrange("q u v -> q v u"))
        last_terms = {n: keep.tile([P, 2, P], F32, name="last_terms%d" % n, tag="term", bufs=3, align_bytes=64) for n in late_tiles}
        for n in late_tiles:
            lo, hi = n * P, (n + 1) * P
            for e in range(2):
                nc.vector.tensor_tensor(
                    last_terms[n][:, e, :], h[2 + e][:].indirect(entries(pos_sb[D - 1], lo, hi)), gate_rows[D - 1][:, lo:hi], MULT
                )
        for n in late_tiles:
            nc.vector.tensor_tensor(
                z_bf16[n][:].rearrange("q (v u e) -> q v u e", u=2, e=2)[:, :, 1, :],
                last_terms[n][:].rearrange("q e v -> q v e"),
                partial_back[:, n - LATE // P, :, :].rearrange("q e v -> q v e"),
                ADD,
            )
        for n in list(late_tiles) + list(early_tiles):
            second_layer(n)

        roots = [sbuf("root_term%d" % d, [P, U], F32) for d in range(D)]
        for d in range(D):
            nc.vector.tensor_tensor(roots[d][:], g[:].indirect(nxt_sb[d][:]), gate2_sb[:, d, :], MULT)
        halves = [slice(0, U // 2), slice(U // 2, U)]
        partial = sbuf("partial", [P, U], F32)
        result = [sbuf("result%d" % n, [P, U // 2], F32) for n in range(2)]
        for cols in halves:
            nc.vector.tensor_tensor(partial[:, cols], roots[0][:, cols], roots[1][:, cols], ADD)
        for n, cols in enumerate(halves):
            nc.vector.tensor_tensor(result[n][:], partial[:, cols], roots[2][:, cols], ADD)
            (nc.scalar, nc.sync)[n].dma_start(out=out[:, cols], in_=result[n][:])
